import numpy as np
import ml_dtypes


def mxq(x, axis, fmt="e4m3"):
    dtype, down = {"e4m3": (ml_dtypes.float8_e4m3fn, 7), "e5m2": (ml_dtypes.float8_e5m2, 14)}[fmt]
    v = np.moveaxis(np.asarray(x, np.float32).astype(ml_dtypes.bfloat16).astype(np.float64), axis, -1)
    blocks = v.reshape(v.shape[:-1] + (-1, 32))
    amax = np.abs(blocks).max(-1, keepdims=True)
    byte = np.maximum(np.where(amax > 0, np.frexp(amax)[1] - 1 + 127, 0) - down, 1)
    scale = np.exp2(byte - 127.0)
    codes = (blocks / scale).astype(np.float32).astype(dtype).astype(np.float64)
    return np.moveaxis((codes * scale).reshape(v.shape), -1, axis)


WIDE = False


def mx_kscale(k):
    if not WIDE:
        return np.ones(k)
    levels = np.array([10, -10, 5, -5, 0])
    if k % 512:
        return np.exp2(np.random.permutation(np.resize(levels, k // 32))).repeat(32)
    a = np.empty((k // 512, 16))
    for p in range(k // 512):
        a[p, :8] = np.random.permutation(np.resize(levels, 8))
        for g in range(8):
            far = levels[np.abs(levels - a[p, g]) >= 10]
            a[p, g + 8] = far[np.random.randint(len(far))]
    return np.exp2(a.ravel()).repeat(32)


def f64(x):
    return np.asarray(x).astype(np.float64)


def striped(idx):
    return np.tile(idx.reshape(-1, 16).T, (8, 1)).astype(np.uint16)


def unstriped(offs):
    return offs[:16].T.reshape(-1).astype(np.int64)


E2M1 = np.array([0.0, 0.5, 1.0, 1.5, 2.0, 3.0, 4.0, 6.0, -0.0, -0.5, -1.0, -1.5, -2.0, -3.0, -4.0, -6.0])


def pack_weight(w, fmt):
    k, n = w.shape
    w = f64(np.asarray(w, np.float32).astype(ml_dtypes.bfloat16)).reshape(k // 32, 32, n)
    amax = np.abs(w).max(1)
    if fmt == "e4m3":
        byte = np.frexp(amax)[1] - 1 + 127 - 7
    else:
        mant, ex = np.frexp(amax / 6.0)
        byte = np.where(mant > 0.5, ex, ex - 1) + 127
    byte = np.clip(np.where(amax > 0, byte, 1), 1, 254)
    scaled = (w * np.exp2(127.0 - byte)[:, None, :]).reshape(k, n).astype(np.float32)
    by_word = np.ascontiguousarray(scaled.reshape(k // 512, 128, 4, n).transpose(0, 1, 3, 2))
    if fmt == "e4m3":
        words = by_word.astype(ml_dtypes.float8_e4m3fn).view(np.uint8)
    else:
        c = by_word.astype(ml_dtypes.float4_e2m1fn).view(np.uint8) & 0xF
        words = (c[..., 0::2] | (c[..., 1::2] << 4)).reshape(k // 512, 128, 2 * n)
    return np.ascontiguousarray(words), np.ascontiguousarray(byte.astype(np.uint8).reshape(k // 512, 16, n))


def unpack_weight(words, scales, fmt):
    g, _, n = scales.shape
    words = np.ascontiguousarray(words).reshape(g, 128, n, -1)
    if fmt == "e4m3":
        vals = words.view(ml_dtypes.float8_e4m3fn).astype(np.float64)
    else:
        nib = np.empty((g, 128, n, 4), np.uint8)
        nib[..., 0::2] = words & 0xF
        nib[..., 1::2] = words >> 4
        vals = E2M1[nib]
    vals = vals * np.repeat(np.exp2(scales.astype(np.float64) - 127.0), 8, axis=1)[..., None]
    return vals.transpose(0, 1, 3, 2).reshape(g * 512, n)


def relu2(v):
    return np.maximum(v, 0.0) ** 2


K, T, E, C, H, N = 512, 1024, 24, 128, 512, 128
TOP = 3


def by_expert(wq, xq):
    return np.concatenate([wq[e].T @ xq[:, e * C:(e + 1) * C] for e in range(E)], axis=1)


def setup_inputs():
    n = np.random.standard_normal
    s = mx_kscale(K)[:, None]
    u = mx_kscale(H)
    deal = np.repeat(np.arange(E), C).reshape(TOP, T)[:, np.random.permutation(T)]
    deal = np.take_along_axis(deal, np.argsort(np.random.rand(TOP, T), axis=0), axis=0)
    for _ in range(8):
        s_, t_ = np.random.permutation(T).reshape(2, -1); r = np.random.randint(TOP, size=T // 2); x, y = deal[r, s_].copy(), deal[r, t_].copy()
        ok = ~((deal[:, s_] == y).any(0) | (deal[:, t_] == x).any(0)); deal[r[ok], s_[ok]] = y[ok]; deal[r[ok], t_[ok]] = x[ok]
    order = np.lexsort((np.random.rand(TOP * T), deal.reshape(-1)))
    slot_token = order % T; pos = np.empty(TOP * T, np.int64); pos[order] = np.arange(TOP * T); pos = pos.reshape(TOP, T)
    g = np.random.uniform(0.5, 1.5, (TOP, T)); g = g / g.sum(0)
    w1 = [pack_weight(m, "e2m1") for m in n((E, K, H)) / np.sqrt(K) / s[None] * u[None, None, :]]
    w2 = [pack_weight(m, "e2m1") for m in n((E, H, N)) / np.sqrt(H) / u[None, :, None] ** 2]
    return {
        "xT": (n((K, T)) * s).astype(np.float32),
        "w1_words": np.stack([m[0] for m in w1]),
        "w1_scales": np.stack([m[1] for m in w1]),
        "w2_words": np.stack([m[0] for m in w2]),
        "w2_scales": np.stack([m[1] for m in w2]),
        "gate": np.stack([np.tile(r, (N, 1)) for r in g]).astype(np.float32),
        "offs": striped(slot_token),
        "pos1": striped(pos[0]),
        "pos2": striped(pos[1]),
        "pos3": striped(pos[2]),
    }


def reference(xT, w1_words, w1_scales, w2_words, w2_scales, gate, offs, pos1, pos2, pos3):
    idx = unstriped(offs)
    w1 = np.stack([unpack_weight(w1_words[e], w1_scales[e], "e2m1") for e in range(E)])
    w2 = np.stack([unpack_weight(w2_words[e], w2_scales[e], "e2m1") for e in range(E)])
    xq = mxq(f64(xT)[:, idx], 0, "e4m3")
    h = relu2(by_expert(w1, xq))
    y = by_expert(w2, mxq(h, 0, "e4m3"))
    return sum(f64(gate[r]) * y[:, unstriped(p)] for r, p in enumerate((pos1, pos2, pos3)))

@@ -1,0 +1,235 @@
+from contextlib import ExitStack
+
+import concourse.mybir as mybir
+from concourse.masks import make_identity
+
+K, T, E, C, H, N = 512, 1024, 24, 128, 512, 128
+TOP = 3
+S = E * C
+FLOPS = 2 * S * (K * H + H * N)
+
+F32 = mybir.dt.float32
+BF16 = mybir.dt.bfloat16
+I32 = mybir.dt.int32
+U32 = mybir.dt.uint32
+U16 = mybir.dt.uint16
+U8 = mybir.dt.uint8
+FP8X4 = mybir.dt.float8_e4m3fn_x4
+FP4X4 = mybir.dt.float4_e2m1fn_x4
+ACT = mybir.ActivationFunctionType
+ALU = mybir.AluOpType
+
+P = 128
+PACK = 4
+
+X_LOADS = [0, 512, 768, 1024]
+X_CUTS = [0, 256, 512, 640, 768, 896, 1024]
+X_ON_SCALAR = (0, 2, 4)
+RELU_ON_VECTOR = (3, 5, 7, 9, 10, 11, 13, 15, 17, 19, 20, 21, 22, 23)
+OUT_CUTS = [0, 512, 768, 1024]
+
+
+def tile_moe_tk_mlp_relu2_kernel(
+    tc, xT, w1_words, w1_scales, w2_words, w2_scales, gate, offs, pos1, pos2, pos3, out
+):
+    nc = tc.nc
+    with ExitStack() as ctx:
+        held = ctx.enter_context(tc.tile_pool(name="held", bufs=1))
+        ring = ctx.enter_context(tc.tile_pool(name="ring", bufs=6))
+        ring2 = ctx.enter_context(tc.tile_pool(name="ring2", bufs=2))
+        psum_a = ctx.enter_context(tc.psum_pool(name="psum_a", bufs=3))
+        psum_b = ctx.enter_context(tc.psum_pool(name="psum_b", bufs=3))
+        psum_y = ctx.enter_context(tc.psum_pool(name="psum_y", bufs=2))
+
+        offs_sb = held.tile([P, S // 16], U16, name="offs_sb")
+        pos_sb = [held.tile([P, T // 16], U16, name=f"pos{r}_sb") for r in range(TOP)]
+        x_words = held.tile([P, T], U32, name="x_words", align_bytes=64)
+        x_scales = held.tile([P, T], U8, name="x_scales", align_bytes=64)
+        w1 = held.tile([P, E, 2 * H], U8, name="w1", align_bytes=64)
+        w1s = held.tile([P, E, H], U8, name="w1s", align_bytes=64)
+        w2 = held.tile([P, E, 2 * N], U8, name="w2", align_bytes=64)
+        w2s = held.tile([P, E, N], U8, name="w2s", align_bytes=64)
+        gate_sb = held.tile([P, TOP, T], F32, name="gate_sb")
+        y = held.tile([P, S], F32, name="y")
+        ident = held.tile([P, P], F32, name="ident")
+
+        nc.gpsimd.memset(x_scales[:], 0)
+        make_identity(nc, ident[:])
+        nc.vector.memset(w1s[:, 0:8, :].bitcast(I32), 0)
+        nc.vector.memset(w2s[:, 0:8, :].bitcast(I32), 0)
+        nc.gpsimd.memset(w1s[:, 8:E, :].bitcast(I32), 0)
+        nc.gpsimd.memset(w2s[:, 8:E, :].bitcast(I32), 0)
+
+        x_raw = held.tile([P, PACK, T], F32, name="x_raw")
+        x_view = xT.rearrange("(p j) t -> p j t", j=PACK)
+
+        def load_x(i):
+            cols = slice(X_LOADS[i], X_LOADS[i + 1])
+            nc.sync.dma_start(x_raw[:, :, cols], x_view[:, :, cols])
+
+        def load_w1(a, b):
+            nc.sync.dma_start(
+                w1[:, a:b, :].bitcast(I32), w1_words[a:b, 0].rearrange("e p n -> p e n").bitcast(I32)
+            )
+
+        def load_w2(a, b):
+            nc.sync.dma_start(
+                w2[:, a:b, :].bitcast(I32), w2_words[a:b, 0].rearrange("e p n -> p e n").bitcast(I32)
+            )
+
+        def load_scales(queue, tile, src, a, b):
+            for q in range(4):
+                queue.dma_start(
+                    tile[32 * q : 32 * q + 4, a:b, :].bitcast(I32),
+                    src[a:b, 0, 4 * q : 4 * q + 4, :].rearrange("e q n -> q e n").bitcast(I32),
+                )
+
+        load_scales(nc.gpsimd, w1s, w1_scales, 8, E)
+        load_scales(nc.gpsimd, w2s, w2_scales, 8, E)
+        load_x(0)
+        load_x(1)
+        load_scales(nc.sync, w1s, w1_scales, 0, 8)
+        nc.sync.dma_start(offs_sb[:], offs)
+        load_x(2)
+        load_w1(0, 2)
+        load_scales(nc.sync, w2s, w2_scales, 0, 8)
+        load_w1(2, 6)
+        load_w2(0, 6)
+        load_w1(6, 12)
+        load_w2(6, 14)
+        load_w1(12, 18)
+        load_w2(14, E)
+        load_w1(18, E)
+        for r, p in enumerate((pos1, pos2, pos3)):
+            nc.sync.dma_start(pos_sb[r][:], p)
+        nc.sync.dma_start(gate_sb[:], gate.rearrange("r p t -> p r t"))
+
+        for i in range(len(X_CUTS) - 1):
+            t0, t1 = X_CUTS[i], X_CUTS[i + 1]
+            grouped = held.tile([P, t1 - t0, PACK], BF16, name=f"x_grouped{i}", align_bytes=64)
+            src = x_raw[:, :, t0:t1].rearrange("p j t -> p t j")
+            if i in X_ON_SCALAR:
+                nc.scalar.activation(grouped[:], src, ACT.Copy)
+            else:
+                nc.vector.tensor_copy(grouped[:], src)
+            nc.vector.quantize_mx(
+                out=x_words[:, t0:t1].bitcast(FP8X4),
+                scales=x_scales[:, t0:t1],
+                in_=grouped[:].rearrange("p t j -> p (t j)"),
+            )
+
+        gath = ctx.enter_context(tc.tile_pool(name="gath", bufs=4))
+        gathered = {}
+
+        def gather(e0, n):
+            cols = slice(e0 * C // 16, (e0 + n) * C // 16)
+            gw = gath.tile([P, n * C], U32, name="gw", align_bytes=64)
+            gs = gath.tile([P, n * C], U8, name="gs", align_bytes=64)
+            nc.vector.tensor_copy(gw[:], x_words[:].indirect(offs_sb[:, cols]))
+            nc.vector.tensor_copy(gs[:], x_scales[:].indirect(offs_sb[:, cols]))
+            for e in range(e0, e0 + n):
+                gathered[e] = (gw, gs, (e - e0) * C)
+
+        acts = {}
+        hs = {}
+        y_bank = {}
+
+        def first(e):
+            gw, gs, c0 = gathered[e]
+            a = psum_a.tile([C, H], F32, name="a")
+            nc.tensor.matmul_mx(
+                out=a[:],
+                lhsT=gw[:, c0 : c0 + C].bitcast(FP8X4),
+                lhsT_scale=gs[:, c0 : c0 + C],
+                rhs=w1[:, e, :].bitcast(FP4X4),
+                rhs_scale=w1s[:, e, :],
+                start=True,
+                stop=True,
+            )
+            r = ring.tile([C, PACK, P], F32, name="r")
+            src = a[:].rearrange("s (m t) -> s t m", t=PACK)
+            if e in RELU_ON_VECTOR:
+                nc.vector.tensor_scalar_max(r[:], src, 0.0)
+            else:
+                nc.scalar.activation(r[:], src, ACT.Relu)
+            acts[e] = r
+
+        def turn(e):
+            b = psum_b.tile([P, PACK, C], F32, name="b")
+            for t in range(PACK):
+                nc.tensor.transpose(b[:, t, :], acts[e][:, t, :], ident[:])
+            h = ring.tile([P, C, PACK], BF16, name="h", align_bytes=64)
+            nc.scalar.activation(h[:], b[:].rearrange("p t s -> p s t"), ACT.Square)
+            hs[e] = h
+
+        def second(e):
+            hw = ring.tile([P, C], U32, name="hw", align_bytes=64)
+            hsc = ring.tile([P, C], U8, name="hsc", align_bytes=64)
+            nc.vector.quantize_mx(
+                out=hw[:].bitcast(FP8X4), scales=hsc[:], in_=hs[e][:].rearrange("p s t -> p (s t)")
+            )
+            if e % 4 == 0:
+                y_bank[e // 4] = psum_y.tile([N, 4, C], F32, name="yb")
+            yb = y_bank[e // 4]
+            nc.tensor.matmul_mx(
+                out=yb[:, e % 4, :],
+                lhsT=w2[:, e, :].bitcast(FP4X4),
+                lhsT_scale=w2s[:, e, :],
+                rhs=hw[:].bitcast(FP8X4),
+                rhs_scale=hsc[:],
+                start=True,
+                stop=True,
+            )
+            if e % 4 == 3 or e == E - 3:
+                lo = e - 1 if e >= E - 3 else e - 3
+                nc.scalar.activation(
+                    y[:, lo * C : (e + 1) * C],
+                    yb[:, lo % 4 : e % 4 + 1, :].rearrange("n q s -> n (q s)"),
+                    ACT.Copy,
+                )
+
+        gather(0, 2)
+        gather(2, 2)
+        for step in range(E // 2 + 3):
+            if step >= 3:
+                second(2 * step - 6)
+                second(2 * step - 5)
+            if 1 <= step <= E // 2:
+                turn(2 * step - 2)
+                turn(2 * step - 1)
+            if step < E // 2:
+                first(2 * step)
+                first(2 * step + 1)
+            if step + 2 < E // 2:
+                gather(2 * step + 4, 2)
+
+        prods = {}
+
+        def product(i, r):
+            t0, t1 = OUT_CUTS[i], OUT_CUTS[i + 1]
+            pr = ring2.tile([P, t1 - t0], F32, name=f"pr{r}")
+            nc.vector.tensor_tensor(
+                pr[:], y[:].indirect(pos_sb[r][:, t0 // 16 : t1 // 16]), gate_sb[:, r, t0:t1], ALU.mult
+            )
+            prods[i, r] = pr
+
+        def add01(i):
+            s = ring2.tile([P, OUT_CUTS[i + 1] - OUT_CUTS[i]], F32, name="s01")
+            nc.vector.tensor_tensor(s[:], prods[i, 0][:], prods[i, 1][:], ALU.add)
+            prods[i, 3] = s
+
+        def add2(i):
+            t0, t1 = OUT_CUTS[i], OUT_CUTS[i + 1]
+            s = ring2.tile([P, t1 - t0], F32, name="s012")
+            nc.vector.tensor_tensor(s[:], prods[i, 3][:], prods[i, 2][:], ALU.add)
+            nc.sync.dma_start(out[:, t0:t1], s[:])
+
+        cuts = len(OUT_CUTS) - 1
+        for i in range(cuts):
+            product(i, 0)
+            product(i, 1)
+            if i > 0:
+                add2(i - 1)
+            product(i, 2)
+            add01(i)
+        add2(cuts - 1)

@@ -22,11 +22,16 @@ ALU = mybir.AluOpType
 P = 128
 PACK = 4
 
-X_LOADS = [0, 512, 768, 1024]
-X_CUTS = [0, 256, 512, 640, 768, 896, 1024]
-X_ON_SCALAR = (0, 2, 4)
-RELU_ON_VECTOR = (3, 5, 7, 9, 10, 11, 13, 15, 17, 19, 20, 21, 22, 23)
-OUT_CUTS = [0, 512, 768, 1024]
+X_LOADS = [0,512,768,1024]
+X_CUTS = [[0,256,"S"],[256,512,"V"],[512,640,"S"],[640,768,"V"],[768,896,"V"],[896,1024,"S"]]
+RELU_ON_VECTOR = [3,5,7,11,13,15,19,21,23]
+SQUARE_ON_VECTOR = []
+SCALE_CUTS = [0,8,16,24]
+GATHER_CUTS = [0,2,4,6,8,10,12,14,16,18,20,22,24]
+QUANT_SINGLE = []
+Y_CUTS = [4,8,12,16,20,22,24]
+Y_ON_VECTOR = [8,16,22]
+OUT_CUTS = [0,512,768,1024]
 
 
 def tile_moe_tk_mlp_relu2_kernel(
@@ -37,78 +42,83 @@ def tile_moe_tk_mlp_relu2_kernel(
         held = ctx.enter_context(tc.tile_pool(name="held", bufs=1))
         ring = ctx.enter_context(tc.tile_pool(name="ring", bufs=6))
         ring2 = ctx.enter_context(tc.tile_pool(name="ring2", bufs=2))
-        psum_a = ctx.enter_context(tc.psum_pool(name="psum_a", bufs=3))
+        gath = ctx.enter_context(tc.tile_pool(name="gath", bufs=3))
+        psum_a = ctx.enter_context(tc.psum_pool(name="psum_a", bufs=5))
         psum_b = ctx.enter_context(tc.psum_pool(name="psum_b", bufs=3))
-        psum_y = ctx.enter_context(tc.psum_pool(name="psum_y", bufs=2))
 
         offs_sb = held.tile([P, S // 16], U16, name="offs_sb")
         pos_sb = [held.tile([P, T // 16], U16, name=f"pos{r}_sb") for r in range(TOP)]
         x_words = held.tile([P, T], U32, name="x_words", align_bytes=64)
         x_scales = held.tile([P, T], U8, name="x_scales", align_bytes=64)
-        w1 = held.tile([P, E, 2 * H], U8, name="w1", align_bytes=64)
-        w1s = held.tile([P, E, H], U8, name="w1s", align_bytes=64)
-        w2 = held.tile([P, E, 2 * N], U8, name="w2", align_bytes=64)
+        w1s = [
+            held.tile([P, b - a, H], U8, name=f"w1s{a}", align_bytes=64) for a, b in zip(SCALE_CUTS, SCALE_CUTS[1:])
+        ]
         w2s = held.tile([P, E, N], U8, name="w2s", align_bytes=64)
         gate_sb = held.tile([P, TOP, T], F32, name="gate_sb")
         y = held.tile([P, S], F32, name="y")
         ident = held.tile([P, P], F32, name="ident")
 
-        nc.gpsimd.memset(x_scales[:], 0)
+        nc.vector.memset(w1s[0][:].bitcast(I32), 0)
         make_identity(nc, ident[:])
-        nc.vector.memset(w1s[:, 0:8, :].bitcast(I32), 0)
-        nc.vector.memset(w2s[:, 0:8, :].bitcast(I32), 0)
-        nc.gpsimd.memset(w1s[:, 8:E, :].bitcast(I32), 0)
-        nc.gpsimd.memset(w2s[:, 8:E, :].bitcast(I32), 0)
+        nc.vector.memset(w1s[1][:].bitcast(I32), 0)
+        nc.vector.memset(w2s[:].bitcast(I32), 0)
+        nc.vector.memset(x_scales[:].bitcast(I32), 0)
+        for tile in w1s[2:]:
+            nc.vector.memset(tile[:].bitcast(I32), 0)
 
-        x_raw = held.tile([P, PACK, T], F32, name="x_raw")
+        w1, w2, x_raw = {}, {}, {}
         x_view = xT.rearrange("(p j) t -> p j t", j=PACK)
 
-        def load_x(i):
-            cols = slice(X_LOADS[i], X_LOADS[i + 1])
-            nc.sync.dma_start(x_raw[:, :, cols], x_view[:, :, cols])
+        def load_words(dst, src, width, a, b, queue, tag):
+            tile = held.tile([P, b - a, width], U8, name=tag, tag=tag, align_bytes=64)
+            queue.dma_start(tile[:].bitcast(I32), src[a:b, 0].rearrange("e p n -> p e n").bitcast(I32))
+            for e in range(a, b):
+                dst[e] = tile[:, e - a, :]
 
-        def load_w1(a, b):
-            nc.sync.dma_start(
-                w1[:, a:b, :].bitcast(I32), w1_words[a:b, 0].rearrange("e p n -> p e n").bitcast(I32)
-            )
+        def load_w1(a, b, queue=nc.sync, tag=None):
+            load_words(w1, w1_words, 2 * H, a, b, queue, tag or f"w1_{a}")
 
-        def load_w2(a, b):
-            nc.sync.dma_start(
-                w2[:, a:b, :].bitcast(I32), w2_words[a:b, 0].rearrange("e p n -> p e n").bitcast(I32)
-            )
+        def load_w2(a, b, queue=nc.sync, tag=None):
+            load_words(w2, w2_words, 2 * N, a, b, queue, tag or f"w2_{a}")
 
-        def load_scales(queue, tile, src, a, b):
-            for q in range(4):
+        def load_scales(queue, tile, src):
+            for r in range(4):
                 queue.dma_start(
-                    tile[32 * q : 32 * q + 4, a:b, :].bitcast(I32),
-                    src[a:b, 0, 4 * q : 4 * q + 4, :].rearrange("e q n -> q e n").bitcast(I32),
+                    tile[r:P:32, :, :].bitcast(I32),
+                    src[:, 0, r:16:4, :].rearrange("e q n -> q e n").bitcast(I32),
                 )
 
-        load_scales(nc.gpsimd, w1s, w1_scales, 8, E)
-        load_scales(nc.gpsimd, w2s, w2_scales, 8, E)
-        load_x(0)
-        load_x(1)
-        load_scales(nc.sync, w1s, w1_scales, 0, 8)
+        def load_w1s(i, queue=nc.sync):
+            load_scales(queue, w1s[i], w1_scales[SCALE_CUTS[i] : SCALE_CUTS[i + 1]])
+
+        def load_w2s(a, b, queue=nc.sync):
+            load_scales(queue, w2s[:, a:b, :], w2_scales[a:b])
+
+        for a, b in zip(X_LOADS, X_LOADS[1:]):
+            x_raw[a] = held.tile([P, PACK, b - a], F32, name=f"x_raw{a}", tag=f"x_raw{a}", align_bytes=64)
+            nc.sync.dma_start(x_raw[a][:], x_view[:, :, a:b])
+        load_w1s(0)
         nc.sync.dma_start(offs_sb[:], offs)
-        load_x(2)
-        load_w1(0, 2)
-        load_scales(nc.sync, w2s, w2_scales, 0, 8)
-        load_w1(2, 6)
-        load_w2(0, 6)
-        load_w1(6, 12)
-        load_w2(6, 14)
-        load_w1(12, 18)
-        load_w2(14, E)
-        load_w1(18, E)
+        load_w1(0,2)
+        load_w1(2,4)
+        load_w1(4,8)
+        load_w1s(1)
+        load_w1(8,12)
+        load_w1(12,16)
+        load_w1s(2)
+        load_w1(16,20)
+        load_w1(20,24)
+        load_w2s(0,24)
+        load_w2(0,24)
         for r, p in enumerate((pos1, pos2, pos3)):
             nc.sync.dma_start(pos_sb[r][:], p)
         nc.sync.dma_start(gate_sb[:], gate.rearrange("r p t -> p r t"))
 
-        for i in range(len(X_CUTS) - 1):
-            t0, t1 = X_CUTS[i], X_CUTS[i + 1]
-            grouped = held.tile([P, t1 - t0, PACK], BF16, name=f"x_grouped{i}", align_bytes=64)
-            src = x_raw[:, :, t0:t1].rearrange("p j t -> p t j")
-            if i in X_ON_SCALAR:
+        for t0, t1, engine in X_CUTS:
+            grouped = held.tile([P, t1 - t0, PACK], BF16, name=f"x_grouped{t0}", tag=f"x_grouped{t0}", align_bytes=64)
+            lo = max(a for a in X_LOADS if a <= t0)
+            src = x_raw[lo][:, :, t0 - lo : t1 - lo].rearrange("p j t -> p t j")
+            if engine == "S":
                 nc.scalar.activation(grouped[:], src, ACT.Copy)
             else:
                 nc.vector.tensor_copy(grouped[:], src)
@@ -118,90 +128,118 @@ def tile_moe_tk_mlp_relu2_kernel(
                 in_=grouped[:].rearrange("p t j -> p (t j)"),
             )
 
-        gath = ctx.enter_context(tc.tile_pool(name="gath", bufs=4))
+
         gathered = {}
 
-        def gather(e0, n):
-            cols = slice(e0 * C // 16, (e0 + n) * C // 16)
+        def gather(e0, e1):
+            n = e1 - e0
+            cols = slice(e0 * C // 16, e1 * C // 16)
             gw = gath.tile([P, n * C], U32, name="gw", align_bytes=64)
             gs = gath.tile([P, n * C], U8, name="gs", align_bytes=64)
             nc.vector.tensor_copy(gw[:], x_words[:].indirect(offs_sb[:, cols]))
             nc.vector.tensor_copy(gs[:], x_scales[:].indirect(offs_sb[:, cols]))
-            for e in range(e0, e0 + n):
+            for e in range(e0, e1):
                 gathered[e] = (gw, gs, (e - e0) * C)
 
         acts = {}
         hs = {}
         y_bank = {}
 
-        def first(e):
+        def w1_plane(e):
+            i = max(j for j, a in enumerate(SCALE_CUTS) if a <= e)
+            return w1s[i][:, e - SCALE_CUTS[i], :]
+
+        banks = {}
+
+        def mm1(e):
             gw, gs, c0 = gathered[e]
-            a = psum_a.tile([C, H], F32, name="a")
+            banks[e] = psum_a.tile([C, H], F32, name="a")
             nc.tensor.matmul_mx(
-                out=a[:],
+                out=banks[e][:],
                 lhsT=gw[:, c0 : c0 + C].bitcast(FP8X4),
                 lhsT_scale=gs[:, c0 : c0 + C],
-                rhs=w1[:, e, :].bitcast(FP4X4),
-                rhs_scale=w1s[:, e, :],
+                rhs=w1[e].bitcast(FP4X4),
+                rhs_scale=w1_plane(e),
                 start=True,
                 stop=True,
             )
-            r = ring.tile([C, PACK, P], F32, name="r")
-            src = a[:].rearrange("s (m t) -> s t m", t=PACK)
+
+        def relu(e):
+            acts[e] = ring.tile([C, PACK, P], F32, name="r")
+            src = banks[e][:].rearrange("s (m t) -> s t m", t=PACK)
             if e in RELU_ON_VECTOR:
-                nc.vector.tensor_scalar_max(r[:], src, 0.0)
+                nc.vector.tensor_scalar_max(acts[e][:], src, 0.0)
             else:
-                nc.scalar.activation(r[:], src, ACT.Relu)
-            acts[e] = r
+                nc.scalar.activation(acts[e][:], src, ACT.Relu)
 
         def turn(e):
-            b = psum_b.tile([P, PACK, C], F32, name="b")
+            banks[e] = psum_b.tile([P, PACK, C], F32, name="b")
             for t in range(PACK):
-                nc.tensor.transpose(b[:, t, :], acts[e][:, t, :], ident[:])
-            h = ring.tile([P, C, PACK], BF16, name="h", align_bytes=64)
-            nc.scalar.activation(h[:], b[:].rearrange("p t s -> p s t"), ACT.Square)
-            hs[e] = h
+                nc.tensor.transpose(banks[e][:, t, :], acts[e][:, t, :], ident[:])
 
-        def second(e):
-            hw = ring.tile([P, C], U32, name="hw", align_bytes=64)
-            hsc = ring.tile([P, C], U8, name="hsc", align_bytes=64)
-            nc.vector.quantize_mx(
-                out=hw[:].bitcast(FP8X4), scales=hsc[:], in_=hs[e][:].rearrange("p s t -> p (s t)")
-            )
-            if e % 4 == 0:
-                y_bank[e // 4] = psum_y.tile([N, 4, C], F32, name="yb")
-            yb = y_bank[e // 4]
+        def square(e):
+            if e % 2 == 0:
+                hs[e // 2] = ring.tile([P, 2, C, PACK], BF16, name="h", align_bytes=64)
+            nc.scalar.activation(hs[e // 2][:, e % 2], banks[e][:].rearrange("p t s -> p s t"), ACT.Square)
+
+        codes = {}
+
+        def quant(e):
+            if e % 2 == 0:
+                hw = ring.tile([P, 2 * C], U32, name="hw", bufs=12, align_bytes=64)
+                hsc = ring.tile([P, 2 * C], U8, name="hsc", bufs=12, align_bytes=64)
+                codes[e // 2] = (hw, hsc)
+            hw, hsc = codes[e // 2]
+            if e in QUANT_SINGLE:
+                cols = slice(e % 2 * C, (e % 2 + 1) * C)
+                nc.vector.quantize_mx(
+                    out=hw[:, cols].bitcast(FP8X4),
+                    scales=hsc[:, cols],
+                    in_=hs[e // 2][:, e % 2].rearrange("p s t -> p (s t)"),
+                )
+            elif e % 2 == 0:
+                nc.vector.quantize_mx(
+                    out=hw[:].bitcast(FP8X4), scales=hsc[:], in_=hs[e // 2][:].rearrange("p e s t -> p (e s t)")
+                )
+
+        def y_group(e):
+            return max(c for c in [0] + Y_CUTS if c <= e)
+
+        def mm2(e):
+            hw, hsc = codes[e // 2]
+            cols = slice(e % 2 * C, (e % 2 + 1) * C)
+            lo = y_group(e)
+            if e == lo:
+                y_bank[lo] = psum_a.tile([N, 4, C], F32, name="yb", tag="a")
             nc.tensor.matmul_mx(
-                out=yb[:, e % 4, :],
-                lhsT=w2[:, e, :].bitcast(FP4X4),
+                out=y_bank[lo][:, e - lo, :],
+                lhsT=w2[e].bitcast(FP4X4),
                 lhsT_scale=w2s[:, e, :],
-                rhs=hw[:].bitcast(FP8X4),
-                rhs_scale=hsc[:],
+                rhs=hw[:, cols].bitcast(FP8X4),
+                rhs_scale=hsc[:, cols],
                 start=True,
                 stop=True,
             )
-            if e % 4 == 3 or e == E - 3:
-                lo = e - 1 if e >= E - 3 else e - 3
-                nc.scalar.activation(
-                    y[:, lo * C : (e + 1) * C],
-                    yb[:, lo % 4 : e % 4 + 1, :].rearrange("n q s -> n (q s)"),
-                    ACT.Copy,
-                )
 
-        gather(0, 2)
-        gather(2, 2)
-        for step in range(E // 2 + 3):
-            if step >= 3:
-                second(2 * step - 6)
-                second(2 * step - 5)
-            if 1 <= step <= E // 2:
-                turn(2 * step - 2)
-                turn(2 * step - 1)
-            if step < E // 2:
-                first(2 * step)
-                first(2 * step + 1)
-            if step + 2 < E // 2:
-                gather(2 * step + 4, 2)
+        def ycopy(e):
+            if e + 1 in Y_CUTS:
+                lo = y_group(e)
+                src = y_bank[lo][:, 0 : e + 1 - lo, :].rearrange("n q s -> n (q s)")
+                if e + 1 in Y_ON_VECTOR:
+                    nc.vector.tensor_copy(y[:, lo * C : (e + 1) * C], src)
+                else:
+                    nc.scalar.activation(y[:, lo * C : (e + 1) * C], src, ACT.Copy)
+
+        def gather_at(e):
+            if e in GATHER_CUTS:
+                gather(e, GATHER_CUTS[GATHER_CUTS.index(e) + 1])
+
+        stages = [(relu, 0), (mm1, -1), (square, 1), (gather_at, -2), (turn, 0), (quant, 2), (mm2, 12), (ycopy, 12)]
+        for step in range(-2, E // 2 + 12):
+            for stage, lag in stages:
+                if 0 <= step - lag < E // 2:
+                    stage(2 * (step - lag))
+                    stage(2 * (step - lag) + 1)
 
         prods = {}
 

@@ -155,6 +155,15 @@ def tile_moe_tk_mlp_relu2_kernel(
             gw, gs, c0 = gathered[e]
             banks[e] = psum_a.tile([C, H], F32, name="a")
             nc.tensor.matmul_mx(
+                out=banks[e][:, 0:128],
+                lhsT=gw[:, c0 : c0 + C].bitcast(FP8X4),
+                lhsT_scale=gs[:, c0 : c0 + C],
+                rhs=w1[e][:, 0:256].bitcast(FP4X4),
+                rhs_scale=w1_plane(e)[:, 0:128],
+                start=True,
+                stop=True,
+            )
+            nc.tensor.matmul_mx(
                 out=banks[e][:],
                 lhsT=gw[:, c0 : c0 + C].bitcast(FP8X4),
                 lhsT_scale=gs[:, c0 : c0 + C],

@@ -27,11 +27,11 @@ X_CUTS = [[0,256,"S"],[256,512,"V"],[512,640,"S"],[640,768,"V"],[768,896,"V"],[8
 RELU_ON_VECTOR = [3,5,7,11,13,15,19,21,23]
 SQUARE_ON_VECTOR = []
 SCALE_CUTS = [0,8,16,24]
-GATHER_CUTS = [0,2,4,6,8,10,12,14,16,18,20,22,24]
+GATHER_CUTS = [0,1,2,4,6,8,10,12,14,16,18,20,22,24]
 QUANT_SINGLE = []
 Y_CUTS = [4,8,12,16,20,22,24]
 Y_ON_VECTOR = [8,16,22]
-OUT_CUTS = [0,512,768,1024]
+OUT_CUTS = [0,256,512,768,896,1024]
 
 
 def tile_moe_tk_mlp_relu2_kernel(
@@ -97,8 +97,8 @@ def tile_moe_tk_mlp_relu2_kernel(
         for a, b in zip(X_LOADS, X_LOADS[1:]):
             x_raw[a] = held.tile([P, PACK, b - a], F32, name=f"x_raw{a}", tag=f"x_raw{a}", align_bytes=64)
             nc.sync.dma_start(x_raw[a][:], x_view[:, :, a:b])
-        load_w1s(0)
         nc.sync.dma_start(offs_sb[:], offs)
+        load_w1s(0)
         load_w1(0,2)
         load_w1(2,4)
         load_w1(4,8)
@@ -254,11 +254,30 @@ def tile_moe_tk_mlp_relu2_kernel(
 
         def product(i, r):
             t0, t1 = OUT_CUTS[i], OUT_CUTS[i + 1]
-            pr = ring2.tile([P, t1 - t0], F32, name=f"pr{r}")
+            prods[i, r] = held.tile([P, t1 - t0], F32, name=f"pr{i}_{r}")
             nc.vector.tensor_tensor(
-                pr[:], y[:].indirect(pos_sb[r][:, t0 // 16 : t1 // 16]), gate_sb[:, r, t0:t1], ALU.mult
+                prods[i, r][:], y[:].indirect(pos_sb[r][:, t0 // 16 : t1 // 16]), gate_sb[:, r, t0:t1], ALU.mult
             )
-            prods[i, r] = pr
+
+        def add_on_tensor(i):
+            t0, t1 = OUT_CUTS[i], OUT_CUTS[i + 1]
+            blocks = (t1 - t0) // P
+            turned = held.tile([P, blocks, P], F32, name=f"turned{i}")
+            sums = [psum_a.tile([P, P], F32, name="sums", tag="a") for c in range(blocks)]
+            for r in range(TOP):
+                for c in range(blocks):
+                    nc.tensor.matmul(
+                        sums[c][:], prods[i, r][:, c * P : (c + 1) * P], ident[:],
+                        start=r == 0, stop=r == TOP - 1, is_transpose=True,
+                    )
+            for c in range(blocks):
+                nc.scalar.activation(turned[:, c, :], sums[c][:], ACT.Copy)
+            back = psum_b.tile([P, blocks, P], F32, name="back", tag="b")
+            for c in range(blocks):
+                nc.tensor.transpose(back[:, c, :], turned[:, c, :], ident[:])
+            result = held.tile([P, blocks, P], F32, name=f"result{i}")
+            nc.scalar.activation(result[:], back[:], ACT.Copy)
+            nc.scalar.dma_start(out[:, t0:t1], result[:].rearrange("n c t -> n (c t)"))
 
         def add01(i):
             s = ring2.tile([P, OUT_CUTS[i + 1] - OUT_CUTS[i]], F32, name="s01")
@@ -275,8 +294,11 @@ def tile_moe_tk_mlp_relu2_kernel(
         for i in range(cuts):
             product(i, 0)
             product(i, 1)
-            if i > 0:
+            if i > 3:
                 add2(i - 1)
             product(i, 2)
-            add01(i)
+            if i < 3:
+                add_on_tensor(i)
+            else:
+                add01(i)
         add2(cuts - 1)

@@ -22,15 +22,24 @@ ALU = mybir.AluOpType
 P = 128
 PACK = 4
 
-X_LOADS = [0,512,768,1024]
-X_CUTS = [[0,256,"S"],[256,512,"V"],[512,640,"S"],[640,768,"V"],[768,896,"V"],[896,1024,"S"]]
-RELU_ON_VECTOR = [3,5,7,11,13,15,19,21,23]
+X_LOADS = [0,512,768,896,1024]
+X_CUTS = [[0,256,"S"],[256,512,"V"],[512,640,"S"],[640,768,"V"],[768,896,"S"],[896,960,"V"],[960,1024,"S"]]
+RELU_ON_VECTOR = [5,7,11,13,15,19,21,22,23]
 SQUARE_ON_VECTOR = []
 SCALE_CUTS = [0,8,16,24]
 GATHER_CUTS = [0,1,2,4,6,8,10,12,14,16,18,20,22,24]
-QUANT_SINGLE = []
+QUANT_SINGLE = [20,21,22,23]
 Y_CUTS = [4,8,12,16,20,22,24]
-Y_ON_VECTOR = [8,16,22]
+Y_ON_VECTOR = [8,16,24]
+WARM = range(0, 24)
+WIDE = range(0, 0)
+PREWARM = 0
+W1_CUTS = [0,2,4,8,12,16,20,24]
+SQ_LAG = 1
+TURN_LAG = 0
+Q_LAG = 2
+Y_STEPS = [14,14,14,14,14,14,14]
+Y_BEFORE = 4
 OUT_CUTS = [0,256,512,768,896,1024]
 
 
@@ -66,6 +75,13 @@ def tile_moe_tk_mlp_relu2_kernel(
         for tile in w1s[2:]:
             nc.vector.memset(tile[:].bitcast(I32), 0)
 
+        if PREWARM:
+            ones = held.tile([P, PACK * C], BF16, name="ones", align_bytes=64)
+            ones_words = held.tile([P, C], U32, name="ones_words", align_bytes=64)
+            ones_scales = held.tile([P, C], U8, name="ones_scales", align_bytes=64)
+            nc.vector.memset(ones[:], 1.0)
+            nc.vector.quantize_mx(out=ones_words[:].bitcast(FP8X4), scales=ones_scales[:], in_=ones[:])
+
         w1, w2, x_raw = {}, {}, {}
         x_view = xT.rearrange("(p j) t -> p j t", j=PACK)
 
@@ -98,16 +114,10 @@ def tile_moe_tk_mlp_relu2_kernel(
             x_raw[a] = held.tile([P, PACK, b - a], F32, name=f"x_raw{a}", tag=f"x_raw{a}", align_bytes=64)
             nc.sync.dma_start(x_raw[a][:], x_view[:, :, a:b])
         nc.sync.dma_start(offs_sb[:], offs)
-        load_w1s(0)
-        load_w1(0,2)
-        load_w1(2,4)
-        load_w1(4,8)
-        load_w1s(1)
-        load_w1(8,12)
-        load_w1(12,16)
-        load_w1s(2)
-        load_w1(16,20)
-        load_w1(20,24)
+        for a, b in zip(W1_CUTS, W1_CUTS[1:]):
+            if a in SCALE_CUTS:
+                load_w1s(SCALE_CUTS.index(a))
+            load_w1(a, b)
         load_w2s(0,24)
         load_w2(0,24)
         for r, p in enumerate((pos1, pos2, pos3)):
@@ -117,11 +127,12 @@ def tile_moe_tk_mlp_relu2_kernel(
         for t0, t1, engine in X_CUTS:
             grouped = held.tile([P, t1 - t0, PACK], BF16, name=f"x_grouped{t0}", tag=f"x_grouped{t0}", align_bytes=64)
             lo = max(a for a in X_LOADS if a <= t0)
-            src = x_raw[lo][:, :, t0 - lo : t1 - lo].rearrange("p j t -> p t j")
+            src = x_raw[lo][:, :, t0 - lo : t1 - lo].rearrange("p j (c i) -> p c j i", i=4)
+            dst = grouped[:].rearrange("p (c i) j -> p c j i", i=4)
             if engine == "S":
-                nc.scalar.activation(grouped[:], src, ACT.Copy)
+                nc.scalar.activation(dst, src, ACT.Copy)
             else:
-                nc.vector.tensor_copy(grouped[:], src)
+                nc.vector.tensor_copy(dst, src)
             nc.vector.quantize_mx(
                 out=x_words[:, t0:t1].bitcast(FP8X4),
                 scales=x_scales[:, t0:t1],
@@ -151,18 +162,33 @@ def tile_moe_tk_mlp_relu2_kernel(
 
         banks = {}
 
+        if PREWARM:
+            scrap = psum_b.tile([C, H], F32, name="scrap", tag="b")
+            for k in range(PREWARM):
+                nc.tensor.matmul_mx(
+                    out=scrap[:],
+                    lhsT=ones_words[:].bitcast(FP8X4),
+                    lhsT_scale=ones_scales[:],
+                    rhs=w1[0].bitcast(FP4X4),
+                    rhs_scale=w1_plane(0),
+                    start=True,
+                    stop=True,
+                )
+
         def mm1(e):
             gw, gs, c0 = gathered[e]
             banks[e] = psum_a.tile([C, H], F32, name="a")
-            nc.tensor.matmul_mx(
-                out=banks[e][:, 0:128],
-                lhsT=gw[:, c0 : c0 + C].bitcast(FP8X4),
-                lhsT_scale=gs[:, c0 : c0 + C],
-                rhs=w1[e][:, 0:256].bitcast(FP4X4),
-                rhs_scale=w1_plane(e)[:, 0:128],
-                start=True,
-                stop=True,
-            )
+            if e in WARM:
+                w = 256 if e in WIDE else 128
+                nc.tensor.matmul_mx(
+                    out=banks[e][:, 0:w],
+                    lhsT=gw[:, c0 : c0 + C].bitcast(FP8X4),
+                    lhsT_scale=gs[:, c0 : c0 + C],
+                    rhs=w1[e][:, 0 : 2 * w].bitcast(FP4X4),
+                    rhs_scale=w1_plane(e)[:, 0:w],
+                    start=True,
+                    stop=True,
+                )
             nc.tensor.matmul_mx(
                 out=banks[e][:],
                 lhsT=gw[:, c0 : c0 + C].bitcast(FP8X4),
@@ -243,9 +269,19 @@ def tile_moe_tk_mlp_relu2_kernel(
             if e in GATHER_CUTS:
                 gather(e, GATHER_CUTS[GATHER_CUTS.index(e) + 1])
 
-        stages = [(relu, 0), (mm1, -1), (square, 1), (gather_at, -2), (turn, 0), (quant, 2), (mm2, 12), (ycopy, 12)]
+        def second(g):
+            lo, hi = ([0] + Y_CUTS)[g], Y_CUTS[g]
+            for e in range(lo, hi):
+                mm2(e)
+            ycopy(hi - 1)
+
+        stages = [(relu, 0), (mm1, -1), (square, SQ_LAG), (gather_at, -2), (turn, TURN_LAG), (quant, Q_LAG)]
         for step in range(-2, E // 2 + 12):
-            for stage, lag in stages:
+            for k, (stage, lag) in enumerate(stages + [(None, 99)]):
+                if k == Y_BEFORE:
+                    for g, at in enumerate(Y_STEPS):
+                        if at == step:
+                            second(g)
                 if 0 <= step - lag < E // 2:
                     stage(2 * (step - lag))
                     stage(2 * (step - lag) + 1)

@@ -34,13 +34,15 @@ Y_ON_VECTOR = [8,16,24]
 WARM = range(0, 24)
 WIDE = range(0, 0)
 PREWARM = 0
+TURNED = 768
+ON_PE = 2
 W1_CUTS = [0,2,4,8,12,16,20,24]
 SQ_LAG = 1
 TURN_LAG = 0
 Q_LAG = 2
 Y_STEPS = [14,14,14,14,14,14,14]
 Y_BEFORE = 4
-OUT_CUTS = [0,256,512,768,896,1024]
+OUT_CUTS = [0,384,768,896,1024]
 
 
 def tile_moe_tk_mlp_relu2_kernel(
@@ -63,7 +65,8 @@ def tile_moe_tk_mlp_relu2_kernel(
             held.tile([P, b - a, H], U8, name=f"w1s{a}", align_bytes=64) for a, b in zip(SCALE_CUTS, SCALE_CUTS[1:])
         ]
         w2s = held.tile([P, E, N], U8, name="w2s", align_bytes=64)
-        gate_sb = held.tile([P, TOP, T], F32, name="gate_sb")
+        gate_sb = held.tile([P, TOP, T - TURNED], F32, name="gate_sb")
+        gate_t = [held.tile([P, TURNED // P], F32, name=f"gate_t{r}") for r in range(TOP)]
         y = held.tile([P, S], F32, name="y")
         ident = held.tile([P, P], F32, name="ident")
 
@@ -122,7 +125,10 @@ def tile_moe_tk_mlp_relu2_kernel(
         load_w2(0,24)
         for r, p in enumerate((pos1, pos2, pos3)):
             nc.sync.dma_start(pos_sb[r][:], p)
-        nc.sync.dma_start(gate_sb[:], gate.rearrange("r p t -> p r t"))
+        nc.sync.dma_start(gate_sb[:], gate[:, :, TURNED:T].rearrange("r p t -> p r t"))
+        with nc.allow_non_contiguous_dma(reason="one gate value a partition"):
+            for r in range(TOP):
+                nc.sync.dma_start(gate_t[r][:], gate[r, 0, 0:TURNED].rearrange("(b p) -> p b", p=P))
 
         for t0, t1, engine in X_CUTS:
             grouped = held.tile([P, t1 - t0, PACK], BF16, name=f"x_grouped{t0}", tag=f"x_grouped{t0}", align_bytes=64)
@@ -292,7 +298,7 @@ def tile_moe_tk_mlp_relu2_kernel(
             t0, t1 = OUT_CUTS[i], OUT_CUTS[i + 1]
             prods[i, r] = held.tile([P, t1 - t0], F32, name=f"pr{i}_{r}")
             nc.vector.tensor_tensor(
-                prods[i, r][:], y[:].indirect(pos_sb[r][:, t0 // 16 : t1 // 16]), gate_sb[:, r, t0:t1], ALU.mult
+                prods[i, r][:], y[:].indirect(pos_sb[r][:, t0 // 16 : t1 // 16]), gate_sb[:, r, t0 - TURNED : t1 - TURNED], ALU.mult
             )
 
         def add_on_tensor(i):
@@ -315,6 +321,29 @@ def tile_moe_tk_mlp_relu2_kernel(
             nc.scalar.activation(result[:], back[:], ACT.Copy)
             nc.scalar.dma_start(out[:, t0:t1], result[:].rearrange("n c t -> n (c t)"))
 
+        def combine_turned(i):
+            t0, t1 = OUT_CUTS[i], OUT_CUTS[i + 1]
+            blocks = (t1 - t0) // P
+            back = [psum_b.tile([P, P], F32, name="back", tag="b") for c in range(blocks)]
+            for r in range(TOP):
+                picked = held.tile([P, t1 - t0], F32, name=f"picked{i}_{r}")
+                nc.vector.tensor_copy(picked[:], y[:].indirect(pos_sb[r][:, t0 // 16 : t1 // 16]))
+                turned = psum_a.tile([P, blocks, P], F32, name="turned", tag="a")
+                for c in range(blocks):
+                    nc.tensor.transpose(turned[:, c, :], picked[:, c * P : (c + 1) * P], ident[:])
+                gated = held.tile([P, blocks, P], F32, name=f"gated{i}_{r}")
+                for c in range(blocks):
+                    b = t0 // P + c
+                    nc.scalar.activation(gated[:, c, :], turned[:, c, :], ACT.Copy, scale=gate_t[r][:, b : b + 1])
+                for c in range(blocks):
+                    nc.tensor.matmul(
+                        back[c][:], gated[:, c, :], ident[:], start=r == 0, stop=r == TOP - 1, is_transpose=True
+                    )
+            result = held.tile([P, blocks, P], F32, name=f"result{i}")
+            for c in range(blocks):
+                nc.scalar.activation(result[:, c, :], back[c][:], ACT.Copy)
+            nc.scalar.dma_start(out[:, t0:t1], result[:].rearrange("n c t -> n (c t)"))
+
         def add01(i):
             s = ring2.tile([P, OUT_CUTS[i + 1] - OUT_CUTS[i]], F32, name="s01")
             nc.vector.tensor_tensor(s[:], prods[i, 0][:], prods[i, 1][:], ALU.add)
@@ -327,13 +356,16 @@ def tile_moe_tk_mlp_relu2_kernel(
             nc.sync.dma_start(out[:, t0:t1], s[:])
 
         cuts = len(OUT_CUTS) - 1
-        for i in range(cuts):
+        first = OUT_CUTS.index(TURNED)
+        for i in range(first):
+            combine_turned(i)
+        for i in range(first, cuts):
             product(i, 0)
             product(i, 1)
-            if i > 3:
+            if i > ON_PE:
                 add2(i - 1)
             product(i, 2)
-            if i < 3:
+            if i < ON_PE:
                 add_on_tensor(i)
             else:
                 add01(i)

@@ -21,28 +21,42 @@ ALU = mybir.AluOpType
 
 P = 128
 PACK = 4
+LIST_ROWS = 16
+PAIRS = E // 2
 
-X_LOADS = [0,512,768,896,1024]
-X_CUTS = [[0,256,"S"],[256,512,"V"],[512,640,"S"],[640,768,"V"],[768,896,"S"],[896,960,"V"],[960,1024,"S"]]
-RELU_ON_VECTOR = [5,7,11,13,15,19,21,22,23]
-SQUARE_ON_VECTOR = []
-SCALE_CUTS = [0,8,16,24]
-GATHER_CUTS = [0,1,2,4,6,8,10,12,14,16,18,20,22,24]
-QUANT_SINGLE = [20,21,22,23]
-Y_CUTS = [4,8,12,16,20,22,24]
-Y_ON_VECTOR = [8,16,24]
-WARM = range(0, 24)
-WIDE = range(0, 0)
-PREWARM = 0
+X_LOADS = [0, 512, 768, 896, 1024]
+X_COPIES = [
+    (0, 256, "scalar"),
+    (256, 512, "vector"),
+    (512, 640, "scalar"),
+    (640, 768, "vector"),
+    (768, 896, "scalar"),
+    (896, 960, "vector"),
+    (960, 1024, "scalar"),
+]
+W1_LOADS = [0, 2, 4, 8, 12, 16, 20, 24]
+SCALE_EXPERTS = 8
+VECTOR_RELU_FROM = 2
+SCALAR_PAIR_EVERY = 4
+SINGLES_FROM = 20
+Y_GROUPS = list(range(0, SINGLES_FROM, 4)) + list(range(SINGLES_FROM, E + 1, 2))
+VECTOR_Y_EVERY = 8
+WARM_COLUMNS = 128
 TURNED = 768
-ON_PE = 2
-W1_CUTS = [0,2,4,8,12,16,20,24]
-SQ_LAG = 1
-TURN_LAG = 0
-Q_LAG = 2
-Y_STEPS = [14,14,14,14,14,14,14]
-Y_BEFORE = 4
-OUT_CUTS = [0,384,768,896,1024]
+TURNED_GROUP = TURNED // 2
+TURNED_BLOCKS = TURNED_GROUP // P
+BACK_LAG = 2
+
+
+def relu_on_vector(e):
+    pair = e // 2
+    if pair == PAIRS - 1:
+        return True
+    return e % 2 == 1 and pair >= VECTOR_RELU_FROM and pair % SCALAR_PAIR_EVERY != 0
+
+
+def list_columns(first, end):
+    return slice(first // LIST_ROWS, end // LIST_ROWS)
 
 
 def tile_moe_tk_mlp_relu2_kernel(
@@ -52,90 +66,70 @@ def tile_moe_tk_mlp_relu2_kernel(
     with ExitStack() as ctx:
         held = ctx.enter_context(tc.tile_pool(name="held", bufs=1))
         ring = ctx.enter_context(tc.tile_pool(name="ring", bufs=6))
-        ring2 = ctx.enter_context(tc.tile_pool(name="ring2", bufs=2))
+        sums = ctx.enter_context(tc.tile_pool(name="sums", bufs=2))
         gath = ctx.enter_context(tc.tile_pool(name="gath", bufs=3))
         psum_a = ctx.enter_context(tc.psum_pool(name="psum_a", bufs=5))
         psum_b = ctx.enter_context(tc.psum_pool(name="psum_b", bufs=3))
 
-        offs_sb = held.tile([P, S // 16], U16, name="offs_sb")
-        pos_sb = [held.tile([P, T // 16], U16, name=f"pos{r}_sb") for r in range(TOP)]
+        offs_sb = held.tile([P, S // LIST_ROWS], U16, name="offs_sb")
+        pos_sb = [held.tile([P, T // LIST_ROWS], U16, name=f"pos{r}_sb") for r in range(TOP)]
         x_words = held.tile([P, T], U32, name="x_words", align_bytes=64)
         x_scales = held.tile([P, T], U8, name="x_scales", align_bytes=64)
-        w1s = [
-            held.tile([P, b - a, H], U8, name=f"w1s{a}", align_bytes=64) for a, b in zip(SCALE_CUTS, SCALE_CUTS[1:])
+        w1_planes = [
+            held.tile([P, SCALE_EXPERTS, H], U8, name=f"w1s{a}", align_bytes=64) for a in range(0, E, SCALE_EXPERTS)
         ]
-        w2s = held.tile([P, E, N], U8, name="w2s", align_bytes=64)
-        gate_sb = held.tile([P, TOP, T - TURNED], F32, name="gate_sb")
-        gate_t = [held.tile([P, TURNED // P], F32, name=f"gate_t{r}") for r in range(TOP)]
+        w2_plane = held.tile([P, E, N], U8, name="w2s", align_bytes=64)
+        gate_rows = held.tile([P, TOP, T - TURNED], F32, name="gate_rows")
+        gate_turned = [held.tile([P, TURNED // P], F32, name=f"gate_turned{r}") for r in range(TOP)]
         y = held.tile([P, S], F32, name="y")
         ident = held.tile([P, P], F32, name="ident")
 
-        nc.vector.memset(w1s[0][:].bitcast(I32), 0)
+        nc.vector.memset(w1_planes[0][:].bitcast(I32), 0)
         make_identity(nc, ident[:])
-        nc.vector.memset(w1s[1][:].bitcast(I32), 0)
-        nc.vector.memset(w2s[:].bitcast(I32), 0)
+        nc.vector.memset(w1_planes[1][:].bitcast(I32), 0)
+        nc.vector.memset(w2_plane[:].bitcast(I32), 0)
         nc.vector.memset(x_scales[:].bitcast(I32), 0)
-        for tile in w1s[2:]:
-            nc.vector.memset(tile[:].bitcast(I32), 0)
-
-        if PREWARM:
-            ones = held.tile([P, PACK * C], BF16, name="ones", align_bytes=64)
-            ones_words = held.tile([P, C], U32, name="ones_words", align_bytes=64)
-            ones_scales = held.tile([P, C], U8, name="ones_scales", align_bytes=64)
-            nc.vector.memset(ones[:], 1.0)
-            nc.vector.quantize_mx(out=ones_words[:].bitcast(FP8X4), scales=ones_scales[:], in_=ones[:])
+        nc.vector.memset(w1_planes[2][:].bitcast(I32), 0)
 
         w1, w2, x_raw = {}, {}, {}
-        x_view = xT.rearrange("(p j) t -> p j t", j=PACK)
 
-        def load_words(dst, src, width, a, b, queue, tag):
-            tile = held.tile([P, b - a, width], U8, name=tag, tag=tag, align_bytes=64)
-            queue.dma_start(tile[:].bitcast(I32), src[a:b, 0].rearrange("e p n -> p e n").bitcast(I32))
+        def load_words(dst, src, width, a, b, name):
+            tile = held.tile([P, b - a, width], U8, name=name, align_bytes=64)
+            nc.sync.dma_start(tile[:].bitcast(I32), src[a:b, 0].rearrange("e p n -> p e n").bitcast(I32))
             for e in range(a, b):
                 dst[e] = tile[:, e - a, :]
 
-        def load_w1(a, b, queue=nc.sync, tag=None):
-            load_words(w1, w1_words, 2 * H, a, b, queue, tag or f"w1_{a}")
-
-        def load_w2(a, b, queue=nc.sync, tag=None):
-            load_words(w2, w2_words, 2 * N, a, b, queue, tag or f"w2_{a}")
-
-        def load_scales(queue, tile, src):
+        def load_scales(tile, src):
             for r in range(4):
-                queue.dma_start(
+                nc.sync.dma_start(
                     tile[r:P:32, :, :].bitcast(I32),
                     src[:, 0, r:16:4, :].rearrange("e q n -> q e n").bitcast(I32),
                 )
 
-        def load_w1s(i, queue=nc.sync):
-            load_scales(queue, w1s[i], w1_scales[SCALE_CUTS[i] : SCALE_CUTS[i + 1]])
-
-        def load_w2s(a, b, queue=nc.sync):
-            load_scales(queue, w2s[:, a:b, :], w2_scales[a:b])
-
+        x_view = xT.rearrange("(p j) t -> p j t", j=PACK)
         for a, b in zip(X_LOADS, X_LOADS[1:]):
-            x_raw[a] = held.tile([P, PACK, b - a], F32, name=f"x_raw{a}", tag=f"x_raw{a}", align_bytes=64)
+            x_raw[a] = held.tile([P, PACK, b - a], F32, name=f"x_raw{a}", align_bytes=64)
             nc.sync.dma_start(x_raw[a][:], x_view[:, :, a:b])
         nc.sync.dma_start(offs_sb[:], offs)
-        for a, b in zip(W1_CUTS, W1_CUTS[1:]):
-            if a in SCALE_CUTS:
-                load_w1s(SCALE_CUTS.index(a))
-            load_w1(a, b)
-        load_w2s(0,24)
-        load_w2(0,24)
-        for r, p in enumerate((pos1, pos2, pos3)):
-            nc.sync.dma_start(pos_sb[r][:], p)
-        nc.sync.dma_start(gate_sb[:], gate[:, :, TURNED:T].rearrange("r p t -> p r t"))
+        for a, b in zip(W1_LOADS, W1_LOADS[1:]):
+            if a % SCALE_EXPERTS == 0:
+                load_scales(w1_planes[a // SCALE_EXPERTS], w1_scales[a : a + SCALE_EXPERTS])
+            load_words(w1, w1_words, 2 * H, a, b, f"w1_{a}")
+        load_scales(w2_plane[:, :, :], w2_scales[0:E])
+        load_words(w2, w2_words, 2 * N, 0, E, "w2")
+        for r, pos in enumerate((pos1, pos2, pos3)):
+            nc.sync.dma_start(pos_sb[r][:], pos)
+        nc.sync.dma_start(gate_rows[:], gate[:, :, TURNED:T].rearrange("r p t -> p r t"))
         with nc.allow_non_contiguous_dma(reason="one gate value a partition"):
             for r in range(TOP):
-                nc.sync.dma_start(gate_t[r][:], gate[r, 0, 0:TURNED].rearrange("(b p) -> p b", p=P))
+                nc.sync.dma_start(gate_turned[r][:], gate[r, 0, 0:TURNED].rearrange("(b p) -> p b", p=P))
 
-        for t0, t1, engine in X_CUTS:
-            grouped = held.tile([P, t1 - t0, PACK], BF16, name=f"x_grouped{t0}", tag=f"x_grouped{t0}", align_bytes=64)
+        for t0, t1, engine in X_COPIES:
+            grouped = held.tile([P, t1 - t0, PACK], BF16, name=f"x_grouped{t0}", align_bytes=64)
             lo = max(a for a in X_LOADS if a <= t0)
             src = x_raw[lo][:, :, t0 - lo : t1 - lo].rearrange("p j (c i) -> p c j i", i=4)
             dst = grouped[:].rearrange("p (c i) j -> p c j i", i=4)
-            if engine == "S":
+            if engine == "scalar":
                 nc.scalar.activation(dst, src, ACT.Copy)
             else:
                 nc.vector.tensor_copy(dst, src)
@@ -145,228 +139,170 @@ def tile_moe_tk_mlp_relu2_kernel(
                 in_=grouped[:].rearrange("p t j -> p (t j)"),
             )
 
+        gathered, a_bank, relu_out, turned_a, h_pair, h_codes = {}, {}, {}, {}, {}, {}
 
-        gathered = {}
+        def gather(e):
+            if e >= 2 and e % 2 == 1:
+                return
+            count = 1 if e < 2 else 2
+            entries = offs_sb[:, list_columns(e * C, (e + count) * C)]
+            words = gath.tile([P, count * C], U32, name="slot_words", align_bytes=64)
+            scales = gath.tile([P, count * C], U8, name="slot_scales", align_bytes=64)
+            nc.vector.tensor_copy(words[:], x_words[:].indirect(entries))
+            nc.vector.tensor_copy(scales[:], x_scales[:].indirect(entries))
+            for k in range(count):
+                gathered[e + k] = (words[:, k * C : (k + 1) * C], scales[:, k * C : (k + 1) * C])
 
-        def gather(e0, e1):
-            n = e1 - e0
-            cols = slice(e0 * C // 16, e1 * C // 16)
-            gw = gath.tile([P, n * C], U32, name="gw", align_bytes=64)
-            gs = gath.tile([P, n * C], U8, name="gs", align_bytes=64)
-            nc.vector.tensor_copy(gw[:], x_words[:].indirect(offs_sb[:, cols]))
-            nc.vector.tensor_copy(gs[:], x_scales[:].indirect(offs_sb[:, cols]))
-            for e in range(e0, e1):
-                gathered[e] = (gw, gs, (e - e0) * C)
-
-        acts = {}
-        hs = {}
-        y_bank = {}
-
-        def w1_plane(e):
-            i = max(j for j, a in enumerate(SCALE_CUTS) if a <= e)
-            return w1s[i][:, e - SCALE_CUTS[i], :]
-
-        banks = {}
-
-        if PREWARM:
-            scrap = psum_b.tile([C, H], F32, name="scrap", tag="b")
-            for k in range(PREWARM):
+        def first_product(e):
+            words, scales = gathered[e]
+            plane = w1_planes[e // SCALE_EXPERTS][:, e % SCALE_EXPERTS, :]
+            a_bank[e] = psum_a.tile([C, H], F32, name="a")
+            for columns in (WARM_COLUMNS, H):
                 nc.tensor.matmul_mx(
-                    out=scrap[:],
-                    lhsT=ones_words[:].bitcast(FP8X4),
-                    lhsT_scale=ones_scales[:],
-                    rhs=w1[0].bitcast(FP4X4),
-                    rhs_scale=w1_plane(0),
+                    out=a_bank[e][:, 0:columns],
+                    lhsT=words.bitcast(FP8X4),
+                    lhsT_scale=scales,
+                    rhs=w1[e][:, 0 : 2 * columns].bitcast(FP4X4),
+                    rhs_scale=plane[:, 0:columns],
                     start=True,
                     stop=True,
                 )
-
-        def mm1(e):
-            gw, gs, c0 = gathered[e]
-            banks[e] = psum_a.tile([C, H], F32, name="a")
-            if e in WARM:
-                w = 256 if e in WIDE else 128
-                nc.tensor.matmul_mx(
-                    out=banks[e][:, 0:w],
-                    lhsT=gw[:, c0 : c0 + C].bitcast(FP8X4),
-                    lhsT_scale=gs[:, c0 : c0 + C],
-                    rhs=w1[e][:, 0 : 2 * w].bitcast(FP4X4),
-                    rhs_scale=w1_plane(e)[:, 0:w],
-                    start=True,
-                    stop=True,
-                )
-            nc.tensor.matmul_mx(
-                out=banks[e][:],
-                lhsT=gw[:, c0 : c0 + C].bitcast(FP8X4),
-                lhsT_scale=gs[:, c0 : c0 + C],
-                rhs=w1[e].bitcast(FP4X4),
-                rhs_scale=w1_plane(e),
-                start=True,
-                stop=True,
-            )
 
         def relu(e):
-            acts[e] = ring.tile([C, PACK, P], F32, name="r")
-            src = banks[e][:].rearrange("s (m t) -> s t m", t=PACK)
-            if e in RELU_ON_VECTOR:
-                nc.vector.tensor_scalar_max(acts[e][:], src, 0.0)
+            relu_out[e] = ring.tile([C, PACK, P], F32, name="relu_out")
+            src = a_bank[e][:].rearrange("s (m t) -> s t m", t=PACK)
+            if relu_on_vector(e):
+                nc.vector.tensor_scalar_max(relu_out[e][:], src, 0.0)
             else:
-                nc.scalar.activation(acts[e][:], src, ACT.Relu)
+                nc.scalar.activation(relu_out[e][:], src, ACT.Relu)
 
         def turn(e):
-            banks[e] = psum_b.tile([P, PACK, C], F32, name="b")
+            turned_a[e] = psum_b.tile([P, PACK, C], F32, name="b")
             for t in range(PACK):
-                nc.tensor.transpose(banks[e][:, t, :], acts[e][:, t, :], ident[:])
+                nc.tensor.transpose(turned_a[e][:, t, :], relu_out[e][:, t, :], ident[:])
 
         def square(e):
             if e % 2 == 0:
-                hs[e // 2] = ring.tile([P, 2, C, PACK], BF16, name="h", align_bytes=64)
-            nc.scalar.activation(hs[e // 2][:, e % 2], banks[e][:].rearrange("p t s -> p s t"), ACT.Square)
+                h_pair[e // 2] = ring.tile([P, 2, C, PACK], BF16, name="h", align_bytes=64)
+            nc.scalar.activation(h_pair[e // 2][:, e % 2], turned_a[e][:].rearrange("p t s -> p s t"), ACT.Square)
 
-        codes = {}
-
-        def quant(e):
+        def quantise(e):
+            pair = e // 2
             if e % 2 == 0:
-                hw = ring.tile([P, 2 * C], U32, name="hw", bufs=12, align_bytes=64)
-                hsc = ring.tile([P, 2 * C], U8, name="hsc", bufs=12, align_bytes=64)
-                codes[e // 2] = (hw, hsc)
-            hw, hsc = codes[e // 2]
-            if e in QUANT_SINGLE:
+                words = ring.tile([P, 2 * C], U32, name="h_words", bufs=PAIRS, align_bytes=64)
+                scales = ring.tile([P, 2 * C], U8, name="h_scales", bufs=PAIRS, align_bytes=64)
+                h_codes[pair] = (words, scales)
+            words, scales = h_codes[pair]
+            if e >= SINGLES_FROM:
                 cols = slice(e % 2 * C, (e % 2 + 1) * C)
                 nc.vector.quantize_mx(
-                    out=hw[:, cols].bitcast(FP8X4),
-                    scales=hsc[:, cols],
-                    in_=hs[e // 2][:, e % 2].rearrange("p s t -> p (s t)"),
+                    out=words[:, cols].bitcast(FP8X4),
+                    scales=scales[:, cols],
+                    in_=h_pair[pair][:, e % 2].rearrange("p s t -> p (s t)"),
                 )
             elif e % 2 == 0:
                 nc.vector.quantize_mx(
-                    out=hw[:].bitcast(FP8X4), scales=hsc[:], in_=hs[e // 2][:].rearrange("p e s t -> p (e s t)")
+                    out=words[:].bitcast(FP8X4),
+                    scales=scales[:],
+                    in_=h_pair[pair][:].rearrange("p e s t -> p (e s t)"),
                 )
 
-        def y_group(e):
-            return max(c for c in [0] + Y_CUTS if c <= e)
-
-        def mm2(e):
-            hw, hsc = codes[e // 2]
-            cols = slice(e % 2 * C, (e % 2 + 1) * C)
-            lo = y_group(e)
-            if e == lo:
-                y_bank[lo] = psum_a.tile([N, 4, C], F32, name="yb", tag="a")
-            nc.tensor.matmul_mx(
-                out=y_bank[lo][:, e - lo, :],
-                lhsT=w2[e].bitcast(FP4X4),
-                lhsT_scale=w2s[:, e, :],
-                rhs=hw[:, cols].bitcast(FP8X4),
-                rhs_scale=hsc[:, cols],
-                start=True,
-                stop=True,
-            )
-
-        def ycopy(e):
-            if e + 1 in Y_CUTS:
-                lo = y_group(e)
-                src = y_bank[lo][:, 0 : e + 1 - lo, :].rearrange("n q s -> n (q s)")
-                if e + 1 in Y_ON_VECTOR:
-                    nc.vector.tensor_copy(y[:, lo * C : (e + 1) * C], src)
-                else:
-                    nc.scalar.activation(y[:, lo * C : (e + 1) * C], src, ACT.Copy)
-
-        def gather_at(e):
-            if e in GATHER_CUTS:
-                gather(e, GATHER_CUTS[GATHER_CUTS.index(e) + 1])
-
-        def second(g):
-            lo, hi = ([0] + Y_CUTS)[g], Y_CUTS[g]
-            for e in range(lo, hi):
-                mm2(e)
-            ycopy(hi - 1)
-
-        stages = [(relu, 0), (mm1, -1), (square, SQ_LAG), (gather_at, -2), (turn, TURN_LAG), (quant, Q_LAG)]
-        for step in range(-2, E // 2 + 12):
-            for k, (stage, lag) in enumerate(stages + [(None, 99)]):
-                if k == Y_BEFORE:
-                    for g, at in enumerate(Y_STEPS):
-                        if at == step:
-                            second(g)
-                if 0 <= step - lag < E // 2:
+        stages = [(relu, 0), (first_product, -1), (square, 1), (gather, -2), (turn, 0), (quantise, 2)]
+        lags = [lag for stage, lag in stages]
+        for step in range(min(lags), PAIRS + max(lags)):
+            for stage, lag in stages:
+                if 0 <= step - lag < PAIRS:
                     stage(2 * (step - lag))
                     stage(2 * (step - lag) + 1)
 
-        prods = {}
+        for lo, hi in zip(Y_GROUPS, Y_GROUPS[1:]):
+            bank = psum_a.tile([N, 4, C], F32, name="y_bank", tag="a")
+            for e in range(lo, hi):
+                words, scales = h_codes[e // 2]
+                cols = slice(e % 2 * C, (e % 2 + 1) * C)
+                nc.tensor.matmul_mx(
+                    out=bank[:, e - lo, :],
+                    lhsT=w2[e].bitcast(FP4X4),
+                    lhsT_scale=w2_plane[:, e, :],
+                    rhs=words[:, cols].bitcast(FP8X4),
+                    rhs_scale=scales[:, cols],
+                    start=True,
+                    stop=True,
+                )
+            src = bank[:, 0 : hi - lo, :].rearrange("n q s -> n (q s)")
+            if hi % VECTOR_Y_EVERY == 0:
+                nc.vector.tensor_copy(y[:, lo * C : hi * C], src)
+            else:
+                nc.scalar.activation(y[:, lo * C : hi * C], src, ACT.Copy)
 
-        def product(i, r):
-            t0, t1 = OUT_CUTS[i], OUT_CUTS[i + 1]
-            prods[i, r] = held.tile([P, t1 - t0], F32, name=f"pr{i}_{r}")
+        gated, back = {}, {}
+
+        def pick_turn_gate(group, r):
+            t0 = group * TURNED_GROUP
+            picked = held.tile([P, TURNED_GROUP], F32, name=f"picked{group}_{r}")
+            nc.vector.tensor_copy(picked[:], y[:].indirect(pos_sb[r][:, list_columns(t0, t0 + TURNED_GROUP)]))
+            turned_y = psum_a.tile([P, TURNED_BLOCKS, P], F32, name="turned_y", tag="a")
+            for c in range(TURNED_BLOCKS):
+                nc.tensor.transpose(turned_y[:, c, :], picked[:, c * P : (c + 1) * P], ident[:])
+            gated[group, r] = held.tile([P, TURNED_BLOCKS, P], F32, name=f"gated{group}_{r}")
+            for c in range(TURNED_BLOCKS):
+                block = group * TURNED_BLOCKS + c
+                nc.scalar.activation(
+                    gated[group, r][:, c, :], turned_y[:, c, :], ACT.Copy, scale=gate_turned[r][:, block : block + 1]
+                )
+
+        def turn_back(group, r):
+            for c in range(TURNED_BLOCKS):
+                if r == 0:
+                    pool, tag = ((psum_b, "b"), (psum_a, "a"))[group]
+                    back[group, c] = pool.tile([P, P], F32, name=f"back{group}", tag=tag)
+                nc.tensor.matmul(
+                    back[group, c][:],
+                    gated[group, r][:, c, :],
+                    ident[:],
+                    start=r == 0,
+                    stop=r == TOP - 1,
+                    is_transpose=True,
+                )
+            if r == TOP - 1:
+                result = held.tile([P, TURNED_BLOCKS, P], F32, name=f"result{group}")
+                for c in range(TURNED_BLOCKS):
+                    nc.scalar.activation(result[:, c, :], back[group, c][:], ACT.Copy)
+                t0 = group * TURNED_GROUP
+                nc.scalar.dma_start(out[:, t0 : t0 + TURNED_GROUP], result[:].rearrange("n c t -> n (c t)"))
+
+        picks = [(group, r) for group in range(TURNED // TURNED_GROUP) for r in range(TOP)]
+        for k in range(len(picks) + BACK_LAG):
+            if k < len(picks):
+                pick_turn_gate(*picks[k])
+            if k >= BACK_LAG:
+                turn_back(*picks[k - BACK_LAG])
+
+        products, partial = {}, {}
+
+        def product(t0, r):
+            products[t0, r] = held.tile([P, P], F32, name=f"product{t0}_{r}")
             nc.vector.tensor_tensor(
-                prods[i, r][:], y[:].indirect(pos_sb[r][:, t0 // 16 : t1 // 16]), gate_sb[:, r, t0 - TURNED : t1 - TURNED], ALU.mult
+                products[t0, r][:],
+                y[:].indirect(pos_sb[r][:, list_columns(t0, t0 + P)]),
+                gate_rows[:, r, t0 - TURNED : t0 - TURNED + P],
+                ALU.mult,
             )
 
-        def add_on_tensor(i):
-            t0, t1 = OUT_CUTS[i], OUT_CUTS[i + 1]
-            blocks = (t1 - t0) // P
-            turned = held.tile([P, blocks, P], F32, name=f"turned{i}")
-            sums = [psum_a.tile([P, P], F32, name="sums", tag="a") for c in range(blocks)]
-            for r in range(TOP):
-                for c in range(blocks):
-                    nc.tensor.matmul(
-                        sums[c][:], prods[i, r][:, c * P : (c + 1) * P], ident[:],
-                        start=r == 0, stop=r == TOP - 1, is_transpose=True,
-                    )
-            for c in range(blocks):
-                nc.scalar.activation(turned[:, c, :], sums[c][:], ACT.Copy)
-            back = psum_b.tile([P, blocks, P], F32, name="back", tag="b")
-            for c in range(blocks):
-                nc.tensor.transpose(back[:, c, :], turned[:, c, :], ident[:])
-            result = held.tile([P, blocks, P], F32, name=f"result{i}")
-            nc.scalar.activation(result[:], back[:], ACT.Copy)
-            nc.scalar.dma_start(out[:, t0:t1], result[:].rearrange("n c t -> n (c t)"))
+        def add_first_two(t0):
+            partial[t0] = sums.tile([P, P], F32, name="partial")
+            nc.vector.tensor_tensor(partial[t0][:], products[t0, 0][:], products[t0, 1][:], ALU.add)
 
-        def combine_turned(i):
-            t0, t1 = OUT_CUTS[i], OUT_CUTS[i + 1]
-            blocks = (t1 - t0) // P
-            back = [psum_b.tile([P, P], F32, name="back", tag="b") for c in range(blocks)]
-            for r in range(TOP):
-                picked = held.tile([P, t1 - t0], F32, name=f"picked{i}_{r}")
-                nc.vector.tensor_copy(picked[:], y[:].indirect(pos_sb[r][:, t0 // 16 : t1 // 16]))
-                turned = psum_a.tile([P, blocks, P], F32, name="turned", tag="a")
-                for c in range(blocks):
-                    nc.tensor.transpose(turned[:, c, :], picked[:, c * P : (c + 1) * P], ident[:])
-                gated = held.tile([P, blocks, P], F32, name=f"gated{i}_{r}")
-                for c in range(blocks):
-                    b = t0 // P + c
-                    nc.scalar.activation(gated[:, c, :], turned[:, c, :], ACT.Copy, scale=gate_t[r][:, b : b + 1])
-                for c in range(blocks):
-                    nc.tensor.matmul(
-                        back[c][:], gated[:, c, :], ident[:], start=r == 0, stop=r == TOP - 1, is_transpose=True
-                    )
-            result = held.tile([P, blocks, P], F32, name=f"result{i}")
-            for c in range(blocks):
-                nc.scalar.activation(result[:, c, :], back[c][:], ACT.Copy)
-            nc.scalar.dma_start(out[:, t0:t1], result[:].rearrange("n c t -> n (c t)"))
+        def add_third_and_store(t0):
+            total = sums.tile([P, P], F32, name="total")
+            nc.vector.tensor_tensor(total[:], partial[t0][:], products[t0, 2][:], ALU.add)
+            nc.sync.dma_start(out[:, t0 : t0 + P], total[:])
 
-        def add01(i):
-            s = ring2.tile([P, OUT_CUTS[i + 1] - OUT_CUTS[i]], F32, name="s01")
-            nc.vector.tensor_tensor(s[:], prods[i, 0][:], prods[i, 1][:], ALU.add)
-            prods[i, 3] = s
-
-        def add2(i):
-            t0, t1 = OUT_CUTS[i], OUT_CUTS[i + 1]
-            s = ring2.tile([P, t1 - t0], F32, name="s012")
-            nc.vector.tensor_tensor(s[:], prods[i, 3][:], prods[i, 2][:], ALU.add)
-            nc.sync.dma_start(out[:, t0:t1], s[:])
-
-        cuts = len(OUT_CUTS) - 1
-        first = OUT_CUTS.index(TURNED)
-        for i in range(first):
-            combine_turned(i)
-        for i in range(first, cuts):
-            product(i, 0)
-            product(i, 1)
-            if i > ON_PE:
-                add2(i - 1)
-            product(i, 2)
-            if i < ON_PE:
-                add_on_tensor(i)
-            else:
-                add01(i)
-        add2(cuts - 1)
+        for t0 in range(TURNED, T, P):
+            product(t0, 0)
+            product(t0, 1)
+            if t0 > TURNED:
+                add_third_and_store(t0 - P)
+            product(t0, 2)
+            add_first_two(t0)
+        add_third_and_store(T - P)

@@ -184,7 +184,9 @@ def tile_moe_tk_mlp_relu2_kernel(
         def square(e):
             if e % 2 == 0:
                 h_pair[e // 2] = ring.tile([P, 2, C, PACK], BF16, name="h", align_bytes=64)
-            nc.scalar.activation(h_pair[e // 2][:, e % 2], turned_a[e][:].rearrange("p t s -> p s t"), ACT.Square)
+            src = turned_a[e][:].rearrange("p t (c i) -> p c t i", i=4)
+            dst = h_pair[e // 2][:, e % 2].rearrange("p (c i) t -> p c t i", i=4)
+            nc.scalar.activation(dst, src, ACT.Square)
 
         def quantise(e):
             pair = e // 2
@@ -298,11 +300,13 @@ def tile_moe_tk_mlp_relu2_kernel(
             nc.vector.tensor_tensor(total[:], partial[t0][:], products[t0, 2][:], ALU.add)
             nc.sync.dma_start(out[:, t0 : t0 + P], total[:])
 
-        for t0 in range(TURNED, T, P):
-            product(t0, 0)
-            product(t0, 1)
-            if t0 > TURNED:
-                add_third_and_store(t0 - P)
-            product(t0, 2)
-            add_first_two(t0)
-        add_third_and_store(T - P)
+        first, second = range(TURNED, T, P)
+        for r in range(TOP):
+            product(first, r)
+        product(second, 0)
+        add_first_two(first)
+        product(second, 1)
+        product(second, 2)
+        add_first_two(second)
+        add_third_and_store(first)
+        add_third_and_store(second)

@@ -20,6 +20,30 @@ ACT = mybir.ActivationFunctionType
 ALU = mybir.AluOpType
 
 P = 128
+BANK = 2048
+NA = 5
+A_BANKS = [e % 5 for e in range(24)]
+Y_STEP = [99, 99, 99, 99, 99, 99, 99]
+W_AT = {'w1_0': 20480, 'w1_2': 22528, 'w1_16': 12288, 'w1_20': 16384, 'w2_0': 49152}
+G_AT = {0: 24576, 256: 26624, 512: 28672, 640: 29696, 768: 30720, 896: 0, 960: 4096}
+X_AT = [32768, 40960, 45056, 47104]
+LATE = [('w', 4, 8, 0), ('w', 8, 16, 4096)]
+NB = 3
+BYTE_MEMSETS = [0, 0, 0, 0, 0]
+GATH = 3
+RING = 6
+LAGS = [0, -1, 1, -2, 0, 2]
+Y_LAG = 99
+Y_BANKS = [4, 0, 1, 2, 3, 4, 0]
+Y_VECTOR = [1, 3, 6]
+V_RELU = [5, 7, 11, 13, 15, 19, 21, 22, 23]
+WARM = list(range(24))
+X_ORDER = [1, 0, 3, 2, 4, 5, 6]
+Q_LAG = 1
+LOADS = ['w0', 's0', 'w2', 's8', 's16', 'w16', 'w20', 't0', 'v0']
+T_BANKS = [1, 2, 3, 4, 0, 1]
+BACK_BANKS = [5, 6, 7, 2, 3, 4]
+GATHER_FROM = [0, 1, 2, 4, 6, 8, 10, 12, 14, 16, 18, 20, 22, 24]
 PACK = 4
 LIST_ROWS = 16
 PAIRS = E // 2
@@ -49,10 +73,7 @@ BACK_LAG = 2
 
 
 def relu_on_vector(e):
-    pair = e // 2
-    if pair == PAIRS - 1:
-        return True
-    return e % 2 == 1 and pair >= VECTOR_RELU_FROM and pair % SCALAR_PAIR_EVERY != 0
+    return e in V_RELU
 
 
 def list_columns(first, end):
@@ -65,36 +86,35 @@ def tile_moe_tk_mlp_relu2_kernel(
     nc = tc.nc
     with ExitStack() as ctx:
         held = ctx.enter_context(tc.tile_pool(name="held", bufs=1))
-        ring = ctx.enter_context(tc.tile_pool(name="ring", bufs=6))
+        ring = ctx.enter_context(tc.tile_pool(name="ring", bufs=RING))
+        stage = ctx.enter_context(tc.tile_pool(name="stage", bufs=1))
         sums = ctx.enter_context(tc.tile_pool(name="sums", bufs=2))
-        gath = ctx.enter_context(tc.tile_pool(name="gath", bufs=3))
-        psum_a = ctx.enter_context(tc.psum_pool(name="psum_a", bufs=5))
-        psum_b = ctx.enter_context(tc.psum_pool(name="psum_b", bufs=3))
+        gath = ctx.enter_context(tc.tile_pool(name="gath", bufs=GATH))
+        psum = ctx.enter_context(tc.psum_pool(name="psum", bufs=1))
+
+        def bank(shape, number, name):
+            return psum.tile(shape, F32, name=name, offset=number * BANK)
 
         offs_sb = held.tile([P, S // LIST_ROWS], U16, name="offs_sb")
         pos_sb = [held.tile([P, T // LIST_ROWS], U16, name=f"pos{r}_sb") for r in range(TOP)]
         x_words = held.tile([P, T], U32, name="x_words", align_bytes=64)
         x_scales = held.tile([P, T], U8, name="x_scales", align_bytes=64)
-        w1_planes = [
-            held.tile([P, SCALE_EXPERTS, H], U8, name=f"w1s{a}", align_bytes=64) for a in range(0, E, SCALE_EXPERTS)
-        ]
+        starts = sorted(int(o[1:]) for o in LOADS if o[0] == "s") + [E]
+        w1_planes = {a: held.tile([P, b - a, H], U8, name=f"w1s{a}", align_bytes=64) for a, b in zip(starts, starts[1:])}
         w2_plane = held.tile([P, E, N], U8, name="w2s", align_bytes=64)
         gate_rows = held.tile([P, TOP, T - TURNED], F32, name="gate_rows")
         gate_turned = [held.tile([P, TURNED // P], F32, name=f"gate_turned{r}") for r in range(TOP)]
         y = held.tile([P, S], F32, name="y")
         ident = held.tile([P, P], F32, name="ident")
 
-        nc.vector.memset(w1_planes[0][:].bitcast(I32), 0)
+        for tile in [w1_planes[0], x_scales] + [w1_planes[a] for a in starts[1:-1]] + [w2_plane]:
+            nc.vector.memset(tile[:].bitcast(I32), 0)
         make_identity(nc, ident[:])
-        nc.vector.memset(w1_planes[1][:].bitcast(I32), 0)
-        nc.vector.memset(w2_plane[:].bitcast(I32), 0)
-        nc.vector.memset(x_scales[:].bitcast(I32), 0)
-        nc.vector.memset(w1_planes[2][:].bitcast(I32), 0)
 
         w1, w2, x_raw = {}, {}, {}
 
         def load_words(dst, src, width, a, b, name):
-            tile = held.tile([P, b - a, width], U8, name=name, align_bytes=64)
+            tile = stage.tile([P, b - a, width], U8, name=name, align_bytes=64, offset=W_AT[name])
             nc.sync.dma_start(tile[:].bitcast(I32), src[a:b, 0].rearrange("e p n -> p e n").bitcast(I32))
             for e in range(a, b):
                 dst[e] = tile[:, e - a, :]
@@ -107,16 +127,21 @@ def tile_moe_tk_mlp_relu2_kernel(
                 )
 
         x_view = xT.rearrange("(p j) t -> p j t", j=PACK)
-        for a, b in zip(X_LOADS, X_LOADS[1:]):
-            x_raw[a] = held.tile([P, PACK, b - a], F32, name=f"x_raw{a}", align_bytes=64)
+        for a, b, at in zip(X_LOADS, X_LOADS[1:], X_AT):
+            x_raw[a] = stage.tile([P, PACK, b - a], F32, name=f"x_raw{a}", align_bytes=64, offset=at)
             nc.sync.dma_start(x_raw[a][:], x_view[:, :, a:b])
         nc.sync.dma_start(offs_sb[:], offs)
-        for a, b in zip(W1_LOADS, W1_LOADS[1:]):
-            if a % SCALE_EXPERTS == 0:
-                load_scales(w1_planes[a // SCALE_EXPERTS], w1_scales[a : a + SCALE_EXPERTS])
-            load_words(w1, w1_words, 2 * H, a, b, f"w1_{a}")
-        load_scales(w2_plane[:, :, :], w2_scales[0:E])
-        load_words(w2, w2_words, 2 * N, 0, E, "w2")
+        for item in LOADS:
+            kind, a = item[0], int(item[1:])
+            b = min([int(o[1:]) for o in LOADS if o[0] == kind and int(o[1:]) > a] + [o[1] for o in LATE if o[0] == kind and o[1] > a] + [E])
+            if kind == "s":
+                load_scales(w1_planes[a], w1_scales[a:b])
+            if kind == "w":
+                load_words(w1, w1_words, 2 * H, a, b, f"w1_{a}")
+            if kind == "t":
+                load_scales(w2_plane[:, a:b, :], w2_scales[a:b])
+            if kind == "v":
+                load_words(w2, w2_words, 2 * N, a, b, f"w2_{a}")
         for r, pos in enumerate((pos1, pos2, pos3)):
             nc.sync.dma_start(pos_sb[r][:], pos)
         nc.sync.dma_start(gate_rows[:], gate[:, :, TURNED:T].rearrange("r p t -> p r t"))
@@ -124,27 +149,44 @@ def tile_moe_tk_mlp_relu2_kernel(
             for r in range(TOP):
                 nc.sync.dma_start(gate_turned[r][:], gate[r, 0, 0:TURNED].rearrange("(b p) -> p b", p=P))
 
-        for t0, t1, engine in X_COPIES:
-            grouped = held.tile([P, t1 - t0, PACK], BF16, name=f"x_grouped{t0}", align_bytes=64)
+        grouped = {}
+
+        def round_x(t0, t1, engine):
+            grouped[t0] = stage.tile([P, t1 - t0, PACK], BF16, name=f"x_grouped{t0}", align_bytes=64, offset=G_AT[t0])
             lo = max(a for a in X_LOADS if a <= t0)
             src = x_raw[lo][:, :, t0 - lo : t1 - lo].rearrange("p j (c i) -> p c j i", i=4)
-            dst = grouped[:].rearrange("p (c i) j -> p c j i", i=4)
+            dst = grouped[t0][:].rearrange("p (c i) j -> p c j i", i=4)
             if engine == "scalar":
                 nc.scalar.activation(dst, src, ACT.Copy)
             else:
                 nc.vector.tensor_copy(dst, src)
+
+        def quantise_x(t0, t1, engine):
             nc.vector.quantize_mx(
                 out=x_words[:, t0:t1].bitcast(FP8X4),
                 scales=x_scales[:, t0:t1],
-                in_=grouped[:].rearrange("p t j -> p (t j)"),
+                in_=grouped[t0][:].rearrange("p t j -> p (t j)"),
             )
+
+        for n in range(len(X_ORDER) + Q_LAG):
+            if n < len(X_ORDER):
+                round_x(*X_COPIES[X_ORDER[n]])
+            if n >= Q_LAG:
+                quantise_x(*X_COPIES[X_ORDER[n - Q_LAG]])
+
+        for kind, a, b, at in LATE:
+            dst, src, width = (w1, w1_words, 2 * H) if kind == "w" else (w2, w2_words, 2 * N)
+            late = stage.tile([P, b - a, width], U8, name=f"late_{kind}{a}", align_bytes=64, offset=at)
+            nc.scalar.dma_start(late[:].bitcast(I32), src[a:b, 0].rearrange("e p n -> p e n").bitcast(I32))
+            for e in range(a, b):
+                dst[e] = late[:, e - a, :]
 
         gathered, a_bank, relu_out, turned_a, h_pair, h_codes = {}, {}, {}, {}, {}, {}
 
         def gather(e):
-            if e >= 2 and e % 2 == 1:
+            if e not in GATHER_FROM:
                 return
-            count = 1 if e < 2 else 2
+            count = GATHER_FROM[GATHER_FROM.index(e) + 1] - e
             entries = offs_sb[:, list_columns(e * C, (e + count) * C)]
             words = gath.tile([P, count * C], U32, name="slot_words", align_bytes=64)
             scales = gath.tile([P, count * C], U8, name="slot_scales", align_bytes=64)
@@ -155,9 +197,10 @@ def tile_moe_tk_mlp_relu2_kernel(
 
         def first_product(e):
             words, scales = gathered[e]
-            plane = w1_planes[e // SCALE_EXPERTS][:, e % SCALE_EXPERTS, :]
-            a_bank[e] = psum_a.tile([C, H], F32, name="a")
-            for columns in (WARM_COLUMNS, H):
+            first = max(a for a in starts if a <= e)
+            plane = w1_planes[first][:, e - first, :]
+            a_bank[e] = bank([C, H], A_BANKS[e], f"a{e}")
+            for columns in (WARM_COLUMNS, H) if e in WARM else (H,):
                 nc.tensor.matmul_mx(
                     out=a_bank[e][:, 0:columns],
                     lhsT=words.bitcast(FP8X4),
@@ -177,7 +220,7 @@ def tile_moe_tk_mlp_relu2_kernel(
                 nc.scalar.activation(relu_out[e][:], src, ACT.Relu)
 
         def turn(e):
-            turned_a[e] = psum_b.tile([P, PACK, C], F32, name="b")
+            turned_a[e] = bank([P, PACK, C], NA + e % NB, f"b{e}")
             for t in range(PACK):
                 nc.tensor.transpose(turned_a[e][:, t, :], relu_out[e][:, t, :], ident[:])
 
@@ -209,21 +252,14 @@ def tile_moe_tk_mlp_relu2_kernel(
                     in_=h_pair[pair][:].rearrange("p e s t -> p (e s t)"),
                 )
 
-        stages = [(relu, 0), (first_product, -1), (square, 1), (gather, -2), (turn, 0), (quantise, 2)]
-        lags = [lag for stage, lag in stages]
-        for step in range(min(lags), PAIRS + max(lags)):
-            for stage, lag in stages:
-                if 0 <= step - lag < PAIRS:
-                    stage(2 * (step - lag))
-                    stage(2 * (step - lag) + 1)
-
-        for lo, hi in zip(Y_GROUPS, Y_GROUPS[1:]):
-            bank = psum_a.tile([N, 4, C], F32, name="y_bank", tag="a")
+        def second(g):
+            lo, hi = Y_GROUPS[g], Y_GROUPS[g + 1]
+            y_bank = bank([N, 4, C], Y_BANKS[g], f"y_bank{g}")
             for e in range(lo, hi):
                 words, scales = h_codes[e // 2]
                 cols = slice(e % 2 * C, (e % 2 + 1) * C)
                 nc.tensor.matmul_mx(
-                    out=bank[:, e - lo, :],
+                    out=y_bank[:, e - lo, :],
                     lhsT=w2[e].bitcast(FP4X4),
                     lhsT_scale=w2_plane[:, e, :],
                     rhs=words[:, cols].bitcast(FP8X4),
@@ -231,11 +267,24 @@ def tile_moe_tk_mlp_relu2_kernel(
                     start=True,
                     stop=True,
                 )
-            src = bank[:, 0 : hi - lo, :].rearrange("n q s -> n (q s)")
-            if hi % VECTOR_Y_EVERY == 0:
+            src = y_bank[:, 0 : hi - lo, :].rearrange("n q s -> n (q s)")
+            if g in Y_VECTOR:
                 nc.vector.tensor_copy(y[:, lo * C : hi * C], src)
             else:
                 nc.scalar.activation(y[:, lo * C : hi * C], src, ACT.Copy)
+
+        stages = list(zip((relu, first_product, square, gather, turn, quantise), LAGS))
+        done = 0
+        for step in range(min(LAGS), PAIRS + max(LAGS)):
+            for stage, lag in stages:
+                if 0 <= step - lag < PAIRS:
+                    stage(2 * (step - lag))
+                    stage(2 * (step - lag) + 1)
+            while done < len(Y_GROUPS) - 1 and Y_STEP[done] <= step:
+                second(done)
+                done += 1
+        for g in range(done, len(Y_GROUPS) - 1):
+            second(g)
 
         gated, back = {}, {}
 
@@ -243,7 +292,7 @@ def tile_moe_tk_mlp_relu2_kernel(
             t0 = group * TURNED_GROUP
             picked = held.tile([P, TURNED_GROUP], F32, name=f"picked{group}_{r}")
             nc.vector.tensor_copy(picked[:], y[:].indirect(pos_sb[r][:, list_columns(t0, t0 + TURNED_GROUP)]))
-            turned_y = psum_a.tile([P, TURNED_BLOCKS, P], F32, name="turned_y", tag="a")
+            turned_y = bank([P, TURNED_BLOCKS, P], T_BANKS[group * TOP + r], f"turned_y{group}_{r}")
             for c in range(TURNED_BLOCKS):
                 nc.tensor.transpose(turned_y[:, c, :], picked[:, c * P : (c + 1) * P], ident[:])
             gated[group, r] = held.tile([P, TURNED_BLOCKS, P], F32, name=f"gated{group}_{r}")
@@ -256,8 +305,7 @@ def tile_moe_tk_mlp_relu2_kernel(
         def turn_back(group, r):
             for c in range(TURNED_BLOCKS):
                 if r == 0:
-                    pool, tag = ((psum_b, "b"), (psum_a, "a"))[group]
-                    back[group, c] = pool.tile([P, P], F32, name=f"back{group}", tag=tag)
+                    back[group, c] = bank([P, P], BACK_BANKS[group * TURNED_BLOCKS + c], f"back{group}_{c}")
                 nc.tensor.matmul(
                     back[group, c][:],
                     gated[group, r][:, c, :],

@@ -20,60 +20,50 @@ ACT = mybir.ActivationFunctionType
 ALU = mybir.AluOpType
 
 P = 128
-BANK = 2048
-NA = 5
-A_BANKS = [e % 5 for e in range(24)]
-Y_STEP = [99, 99, 99, 99, 99, 99, 99]
-W_AT = {'w1_0': 20480, 'w1_2': 22528, 'w1_16': 12288, 'w1_20': 16384, 'w2_0': 49152}
-G_AT = {0: 24576, 256: 26624, 512: 28672, 640: 29696, 768: 30720, 896: 0, 960: 4096}
-X_AT = [32768, 40960, 45056, 47104]
-LATE = [('w', 4, 8, 0), ('w', 8, 16, 4096)]
-NB = 3
-BYTE_MEMSETS = [0, 0, 0, 0, 0]
-GATH = 3
-RING = 6
-LAGS = [0, -1, 1, -2, 0, 2]
-Y_LAG = 99
-Y_BANKS = [4, 0, 1, 2, 3, 4, 0]
-Y_VECTOR = [1, 3, 6]
-V_RELU = [5, 7, 11, 13, 15, 19, 21, 22, 23]
-WARM = list(range(24))
-X_ORDER = [1, 0, 3, 2, 4, 5, 6]
-Q_LAG = 1
-LOADS = ['w0', 's0', 'w2', 's8', 's16', 'w16', 'w20', 't0', 'v0']
-T_BANKS = [1, 2, 3, 4, 0, 1]
-BACK_BANKS = [5, 6, 7, 2, 3, 4]
-GATHER_FROM = [0, 1, 2, 4, 6, 8, 10, 12, 14, 16, 18, 20, 22, 24]
 PACK = 4
 LIST_ROWS = 16
 PAIRS = E // 2
+BANKS = 8
+BANK_BYTES = 2048
+RING = 4
 
 X_LOADS = [0, 512, 768, 896, 1024]
 X_COPIES = [
-    (0, 256, "scalar"),
     (256, 512, "vector"),
-    (512, 640, "scalar"),
+    (0, 256, "scalar"),
     (640, 768, "vector"),
+    (512, 640, "scalar"),
     (768, 896, "scalar"),
     (896, 960, "vector"),
     (960, 1024, "scalar"),
 ]
-W1_LOADS = [0, 2, 4, 8, 12, 16, 20, 24]
 SCALE_EXPERTS = 8
-VECTOR_RELU_FROM = 2
-SCALAR_PAIR_EVERY = 4
-SINGLES_FROM = 20
-Y_GROUPS = list(range(0, SINGLES_FROM, 4)) + list(range(SINGLES_FROM, E + 1, 2))
+VECTOR_RELU_FROM = 3
+H_GROUPS = [0, 8, 16, 20, 22, 23, 24]
+Y_GROUPS = [0, 4, 8, 12, 16, 20, 22, 24]
 VECTOR_Y_EVERY = 8
 WARM_COLUMNS = 128
 TURNED = 768
 TURNED_GROUP = TURNED // 2
 TURNED_BLOCKS = TURNED_GROUP // P
+TURN_BANKS = 3
 BACK_LAG = 2
+
+W1_ROW = 2 * H
+ROUNDED_AT = {896: 0, 960: 4 * W1_ROW}
+LATE_W1_AT = {(4, 8): ROUNDED_AT[896], (8, 16): ROUNDED_AT[960]}
+LAST_W1_AT = {(16, 20): 12 * W1_ROW, (20, 24): 16 * W1_ROW}
+H_WORDS_AT = {0: LAST_W1_AT[16, 20], 8: LAST_W1_AT[20, 24]}
 
 
 def relu_on_vector(e):
-    return e in V_RELU
+    pair = e // 2
+    return pair == PAIRS - 1 or (e % 2 == 1 and pair >= VECTOR_RELU_FROM)
+
+
+def group_of(e, bounds):
+    k = max(k for k, first in enumerate(bounds) if first <= e)
+    return bounds[k], bounds[k + 1]
 
 
 def list_columns(first, end):
@@ -86,36 +76,42 @@ def tile_moe_tk_mlp_relu2_kernel(
     nc = tc.nc
     with ExitStack() as ctx:
         held = ctx.enter_context(tc.tile_pool(name="held", bufs=1))
-        ring = ctx.enter_context(tc.tile_pool(name="ring", bufs=RING))
-        stage = ctx.enter_context(tc.tile_pool(name="stage", bufs=1))
+        shared = ctx.enter_context(tc.tile_pool(name="shared", bufs=1))
+        ring = ctx.enter_context(tc.tile_pool(name="ring", bufs=6))
         sums = ctx.enter_context(tc.tile_pool(name="sums", bufs=2))
-        gath = ctx.enter_context(tc.tile_pool(name="gath", bufs=GATH))
+        gath = ctx.enter_context(tc.tile_pool(name="gath", bufs=3))
         psum = ctx.enter_context(tc.psum_pool(name="psum", bufs=1))
 
-        def bank(shape, number, name):
-            return psum.tile(shape, F32, name=name, offset=number * BANK)
+        def in_bank(number, shape, name):
+            return psum.tile(shape, F32, name=name, offset=number * BANK_BYTES)
+
+        def placed(shape, dtype, name, at):
+            if at is None:
+                return held.tile(shape, dtype, name=name, align_bytes=64)
+            return shared.tile(shape, dtype, name=name, align_bytes=64, offset=at)
 
         offs_sb = held.tile([P, S // LIST_ROWS], U16, name="offs_sb")
         pos_sb = [held.tile([P, T // LIST_ROWS], U16, name=f"pos{r}_sb") for r in range(TOP)]
         x_words = held.tile([P, T], U32, name="x_words", align_bytes=64)
         x_scales = held.tile([P, T], U8, name="x_scales", align_bytes=64)
-        starts = sorted(int(o[1:]) for o in LOADS if o[0] == "s") + [E]
-        w1_planes = {a: held.tile([P, b - a, H], U8, name=f"w1s{a}", align_bytes=64) for a, b in zip(starts, starts[1:])}
+        w1_planes = [
+            held.tile([P, SCALE_EXPERTS, H], U8, name=f"w1s{a}", align_bytes=64) for a in range(0, E, SCALE_EXPERTS)
+        ]
         w2_plane = held.tile([P, E, N], U8, name="w2s", align_bytes=64)
         gate_rows = held.tile([P, TOP, T - TURNED], F32, name="gate_rows")
         gate_turned = [held.tile([P, TURNED // P], F32, name=f"gate_turned{r}") for r in range(TOP)]
         y = held.tile([P, S], F32, name="y")
         ident = held.tile([P, P], F32, name="ident")
 
-        for tile in [w1_planes[0], x_scales] + [w1_planes[a] for a in starts[1:-1]] + [w2_plane]:
+        for tile in (w1_planes[0], x_scales, w1_planes[1], w1_planes[2], w2_plane):
             nc.vector.memset(tile[:].bitcast(I32), 0)
         make_identity(nc, ident[:])
 
         w1, w2, x_raw = {}, {}, {}
 
-        def load_words(dst, src, width, a, b, name):
-            tile = stage.tile([P, b - a, width], U8, name=name, align_bytes=64, offset=W_AT[name])
-            nc.sync.dma_start(tile[:].bitcast(I32), src[a:b, 0].rearrange("e p n -> p e n").bitcast(I32))
+        def load_words(queue, dst, src, width, a, b, name, at=None):
+            tile = placed([P, b - a, width], U8, name, at)
+            queue.dma_start(tile[:].bitcast(I32), src[a:b, 0].rearrange("e p n -> p e n").bitcast(I32))
             for e in range(a, b):
                 dst[e] = tile[:, e - a, :]
 
@@ -126,22 +122,23 @@ def tile_moe_tk_mlp_relu2_kernel(
                     src[:, 0, r:16:4, :].rearrange("e q n -> q e n").bitcast(I32),
                 )
 
+        def load_w1_scales(k):
+            load_scales(w1_planes[k], w1_scales[k * SCALE_EXPERTS : (k + 1) * SCALE_EXPERTS])
+
         x_view = xT.rearrange("(p j) t -> p j t", j=PACK)
-        for a, b, at in zip(X_LOADS, X_LOADS[1:], X_AT):
-            x_raw[a] = stage.tile([P, PACK, b - a], F32, name=f"x_raw{a}", align_bytes=64, offset=at)
+        for a, b in zip(X_LOADS, X_LOADS[1:]):
+            x_raw[a] = held.tile([P, PACK, b - a], F32, name=f"x_raw{a}", align_bytes=64)
             nc.sync.dma_start(x_raw[a][:], x_view[:, :, a:b])
         nc.sync.dma_start(offs_sb[:], offs)
-        for item in LOADS:
-            kind, a = item[0], int(item[1:])
-            b = min([int(o[1:]) for o in LOADS if o[0] == kind and int(o[1:]) > a] + [o[1] for o in LATE if o[0] == kind and o[1] > a] + [E])
-            if kind == "s":
-                load_scales(w1_planes[a], w1_scales[a:b])
-            if kind == "w":
-                load_words(w1, w1_words, 2 * H, a, b, f"w1_{a}")
-            if kind == "t":
-                load_scales(w2_plane[:, a:b, :], w2_scales[a:b])
-            if kind == "v":
-                load_words(w2, w2_words, 2 * N, a, b, f"w2_{a}")
+        load_words(nc.sync, w1, w1_words, W1_ROW, 0, 2, "w1_0")
+        load_w1_scales(0)
+        load_words(nc.sync, w1, w1_words, W1_ROW, 2, 4, "w1_2")
+        load_w1_scales(1)
+        load_w1_scales(2)
+        for (a, b), at in LAST_W1_AT.items():
+            load_words(nc.sync, w1, w1_words, W1_ROW, a, b, f"w1_{a}", at)
+        load_scales(w2_plane, w2_scales)
+        load_words(nc.sync, w2, w2_words, 2 * N, 0, E, "w2")
         for r, pos in enumerate((pos1, pos2, pos3)):
             nc.sync.dma_start(pos_sb[r][:], pos)
         nc.sync.dma_start(gate_rows[:], gate[:, :, TURNED:T].rearrange("r p t -> p r t"))
@@ -149,44 +146,40 @@ def tile_moe_tk_mlp_relu2_kernel(
             for r in range(TOP):
                 nc.sync.dma_start(gate_turned[r][:], gate[r, 0, 0:TURNED].rearrange("(b p) -> p b", p=P))
 
-        grouped = {}
+        rounded = {}
 
-        def round_x(t0, t1, engine):
-            grouped[t0] = stage.tile([P, t1 - t0, PACK], BF16, name=f"x_grouped{t0}", align_bytes=64, offset=G_AT[t0])
+        def round_tokens(t0, t1, engine):
+            rounded[t0] = placed([P, t1 - t0, PACK], BF16, f"x_rounded{t0}", ROUNDED_AT.get(t0))
             lo = max(a for a in X_LOADS if a <= t0)
             src = x_raw[lo][:, :, t0 - lo : t1 - lo].rearrange("p j (c i) -> p c j i", i=4)
-            dst = grouped[t0][:].rearrange("p (c i) j -> p c j i", i=4)
+            dst = rounded[t0][:].rearrange("p (c i) j -> p c j i", i=4)
             if engine == "scalar":
                 nc.scalar.activation(dst, src, ACT.Copy)
             else:
                 nc.vector.tensor_copy(dst, src)
 
-        def quantise_x(t0, t1, engine):
+        def quantise_tokens(t0, t1):
             nc.vector.quantize_mx(
                 out=x_words[:, t0:t1].bitcast(FP8X4),
                 scales=x_scales[:, t0:t1],
-                in_=grouped[t0][:].rearrange("p t j -> p (t j)"),
+                in_=rounded[t0][:].rearrange("p t j -> p (t j)"),
             )
 
-        for n in range(len(X_ORDER) + Q_LAG):
-            if n < len(X_ORDER):
-                round_x(*X_COPIES[X_ORDER[n]])
-            if n >= Q_LAG:
-                quantise_x(*X_COPIES[X_ORDER[n - Q_LAG]])
+        for k in range(len(X_COPIES) + 1):
+            if k < len(X_COPIES):
+                round_tokens(*X_COPIES[k])
+            if k > 0:
+                quantise_tokens(*X_COPIES[k - 1][:2])
 
-        for kind, a, b, at in LATE:
-            dst, src, width = (w1, w1_words, 2 * H) if kind == "w" else (w2, w2_words, 2 * N)
-            late = stage.tile([P, b - a, width], U8, name=f"late_{kind}{a}", align_bytes=64, offset=at)
-            nc.scalar.dma_start(late[:].bitcast(I32), src[a:b, 0].rearrange("e p n -> p e n").bitcast(I32))
-            for e in range(a, b):
-                dst[e] = late[:, e - a, :]
+        for (a, b), at in LATE_W1_AT.items():
+            load_words(nc.scalar, w1, w1_words, W1_ROW, a, b, f"w1_{a}", at)
 
-        gathered, a_bank, relu_out, turned_a, h_pair, h_codes = {}, {}, {}, {}, {}, {}
+        gathered, a_bank, relu_out, turned_a, h, h_codes = {}, {}, {}, {}, {}, {}
 
         def gather(e):
-            if e not in GATHER_FROM:
+            if e >= 2 and e % 2 == 1:
                 return
-            count = GATHER_FROM[GATHER_FROM.index(e) + 1] - e
+            count = 1 if e < 2 else 2
             entries = offs_sb[:, list_columns(e * C, (e + count) * C)]
             words = gath.tile([P, count * C], U32, name="slot_words", align_bytes=64)
             scales = gath.tile([P, count * C], U8, name="slot_scales", align_bytes=64)
@@ -197,10 +190,9 @@ def tile_moe_tk_mlp_relu2_kernel(
 
         def first_product(e):
             words, scales = gathered[e]
-            first = max(a for a in starts if a <= e)
-            plane = w1_planes[first][:, e - first, :]
-            a_bank[e] = bank([C, H], A_BANKS[e], f"a{e}")
-            for columns in (WARM_COLUMNS, H) if e in WARM else (H,):
+            plane = w1_planes[e // SCALE_EXPERTS][:, e % SCALE_EXPERTS, :]
+            a_bank[e] = in_bank(e % RING, [C, H], f"a{e}")
+            for columns in (WARM_COLUMNS, H):
                 nc.tensor.matmul_mx(
                     out=a_bank[e][:, 0:columns],
                     lhsT=words.bitcast(FP8X4),
@@ -220,71 +212,63 @@ def tile_moe_tk_mlp_relu2_kernel(
                 nc.scalar.activation(relu_out[e][:], src, ACT.Relu)
 
         def turn(e):
-            turned_a[e] = bank([P, PACK, C], NA + e % NB, f"b{e}")
+            turned_a[e] = in_bank(RING + e % RING, [P, PACK, C], f"turned_a{e}")
             for t in range(PACK):
                 nc.tensor.transpose(turned_a[e][:, t, :], relu_out[e][:, t, :], ident[:])
 
         def square(e):
-            if e % 2 == 0:
-                h_pair[e // 2] = ring.tile([P, 2, C, PACK], BF16, name="h", align_bytes=64)
+            first, end = group_of(e, H_GROUPS)
+            if e == first:
+                h[first] = held.tile([P, end - first, C, PACK], BF16, name=f"h{first}", align_bytes=64)
             src = turned_a[e][:].rearrange("p t (c i) -> p c t i", i=4)
-            dst = h_pair[e // 2][:, e % 2].rearrange("p (c i) t -> p c t i", i=4)
+            dst = h[first][:, e - first].rearrange("p (c i) t -> p c t i", i=4)
             nc.scalar.activation(dst, src, ACT.Square)
 
-        def quantise(e):
-            pair = e // 2
-            if e % 2 == 0:
-                words = ring.tile([P, 2 * C], U32, name="h_words", bufs=PAIRS, align_bytes=64)
-                scales = ring.tile([P, 2 * C], U8, name="h_scales", bufs=PAIRS, align_bytes=64)
-                h_codes[pair] = (words, scales)
-            words, scales = h_codes[pair]
-            if e >= SINGLES_FROM:
-                cols = slice(e % 2 * C, (e % 2 + 1) * C)
-                nc.vector.quantize_mx(
-                    out=words[:, cols].bitcast(FP8X4),
-                    scales=scales[:, cols],
-                    in_=h_pair[pair][:, e % 2].rearrange("p s t -> p (s t)"),
-                )
-            elif e % 2 == 0:
-                nc.vector.quantize_mx(
-                    out=words[:].bitcast(FP8X4),
-                    scales=scales[:],
-                    in_=h_pair[pair][:].rearrange("p e s t -> p (e s t)"),
-                )
+        def quantise(first):
+            end = group_of(first, H_GROUPS)[1]
+            words = placed([P, (end - first) * C], U32, f"h_words{first}", H_WORDS_AT.get(first))
+            scales = held.tile([P, (end - first) * C], U8, name=f"h_scales{first}", align_bytes=64)
+            nc.vector.quantize_mx(
+                out=words[:].bitcast(FP8X4),
+                scales=scales[:],
+                in_=h[first][:].rearrange("p e s t -> p (e s t)"),
+            )
+            for e in range(first, end):
+                cols = slice((e - first) * C, (e - first + 1) * C)
+                h_codes[e] = (words[:, cols], scales[:, cols])
 
-        def second(g):
-            lo, hi = Y_GROUPS[g], Y_GROUPS[g + 1]
-            y_bank = bank([N, 4, C], Y_BANKS[g], f"y_bank{g}")
-            for e in range(lo, hi):
-                words, scales = h_codes[e // 2]
-                cols = slice(e % 2 * C, (e % 2 + 1) * C)
-                nc.tensor.matmul_mx(
-                    out=y_bank[:, e - lo, :],
-                    lhsT=w2[e].bitcast(FP4X4),
-                    lhsT_scale=w2_plane[:, e, :],
-                    rhs=words[:, cols].bitcast(FP8X4),
-                    rhs_scale=scales[:, cols],
-                    start=True,
-                    stop=True,
-                )
-            src = y_bank[:, 0 : hi - lo, :].rearrange("n q s -> n (q s)")
-            if g in Y_VECTOR:
-                nc.vector.tensor_copy(y[:, lo * C : hi * C], src)
-            else:
-                nc.scalar.activation(y[:, lo * C : hi * C], src, ACT.Copy)
-
-        stages = list(zip((relu, first_product, square, gather, turn, quantise), LAGS))
-        done = 0
-        for step in range(min(LAGS), PAIRS + max(LAGS)):
+        stages = [(relu, 0), (first_product, -1), (square, 1), (gather, -2), (turn, 0)]
+        for step in range(min(lag for stage, lag in stages), PAIRS):
             for stage, lag in stages:
                 if 0 <= step - lag < PAIRS:
                     stage(2 * (step - lag))
                     stage(2 * (step - lag) + 1)
-            while done < len(Y_GROUPS) - 1 and Y_STEP[done] <= step:
-                second(done)
-                done += 1
-        for g in range(done, len(Y_GROUPS) - 1):
-            second(g)
+
+        for first in (H_GROUPS[2], H_GROUPS[0], H_GROUPS[1]):
+            quantise(first)
+        square(E - 2)
+        square(E - 1)
+        for first in H_GROUPS[3:-1]:
+            quantise(first)
+
+        for g, (lo, hi) in enumerate(zip(Y_GROUPS, Y_GROUPS[1:])):
+            y_bank = in_bank(g, [N, 4, C], f"y_bank{g}")
+            for e in range(lo, hi):
+                words, scales = h_codes[e]
+                nc.tensor.matmul_mx(
+                    out=y_bank[:, e - lo, :],
+                    lhsT=w2[e].bitcast(FP4X4),
+                    lhsT_scale=w2_plane[:, e, :],
+                    rhs=words.bitcast(FP8X4),
+                    rhs_scale=scales,
+                    start=True,
+                    stop=True,
+                )
+            src = y_bank[:, 0 : hi - lo, :].rearrange("n q s -> n (q s)")
+            if hi % VECTOR_Y_EVERY == 0:
+                nc.vector.tensor_copy(y[:, lo * C : hi * C], src)
+            else:
+                nc.scalar.activation(y[:, lo * C : hi * C], src, ACT.Copy)
 
         gated, back = {}, {}
 
@@ -292,7 +276,7 @@ def tile_moe_tk_mlp_relu2_kernel(
             t0 = group * TURNED_GROUP
             picked = held.tile([P, TURNED_GROUP], F32, name=f"picked{group}_{r}")
             nc.vector.tensor_copy(picked[:], y[:].indirect(pos_sb[r][:, list_columns(t0, t0 + TURNED_GROUP)]))
-            turned_y = bank([P, TURNED_BLOCKS, P], T_BANKS[group * TOP + r], f"turned_y{group}_{r}")
+            turned_y = in_bank((group * TOP + r) % TURN_BANKS, [P, TURNED_BLOCKS, P], f"turned_y{group}_{r}")
             for c in range(TURNED_BLOCKS):
                 nc.tensor.transpose(turned_y[:, c, :], picked[:, c * P : (c + 1) * P], ident[:])
             gated[group, r] = held.tile([P, TURNED_BLOCKS, P], F32, name=f"gated{group}_{r}")
@@ -305,7 +289,8 @@ def tile_moe_tk_mlp_relu2_kernel(
         def turn_back(group, r):
             for c in range(TURNED_BLOCKS):
                 if r == 0:
-                    back[group, c] = bank([P, P], BACK_BANKS[group * TURNED_BLOCKS + c], f"back{group}_{c}")
+                    block = group * TURNED_BLOCKS + c
+                    back[group, c] = in_bank((TURN_BANKS + block) % BANKS, [P, P], f"back{block}")
                 nc.tensor.matmul(
                     back[group, c][:],
                     gated[group, r][:, c, :],

@@ -40,9 +40,8 @@ X_COPIES = [
 SCALE_EXPERTS = 8
 VECTOR_RELU_FROM = 3
 H_GROUPS = [0, 8, 16, 20, 22, 23, 24]
-Y_GROUPS = [0, 4, 8, 12, 16, 20, 22, 24]
+Y_GROUPS = [0, 4, 8, 12, 16, 20, 23, 24]
 VECTOR_Y_EVERY = 8
-WARM_COLUMNS = 128
 TURNED = 768
 TURNED_GROUP = TURNED // 2
 TURNED_BLOCKS = TURNED_GROUP // P
@@ -190,18 +189,16 @@ def tile_moe_tk_mlp_relu2_kernel(
 
         def first_product(e):
             words, scales = gathered[e]
-            plane = w1_planes[e // SCALE_EXPERTS][:, e % SCALE_EXPERTS, :]
             a_bank[e] = in_bank(e % RING, [C, H], f"a{e}")
-            for columns in (WARM_COLUMNS, H):
-                nc.tensor.matmul_mx(
-                    out=a_bank[e][:, 0:columns],
-                    lhsT=words.bitcast(FP8X4),
-                    lhsT_scale=scales,
-                    rhs=w1[e][:, 0 : 2 * columns].bitcast(FP4X4),
-                    rhs_scale=plane[:, 0:columns],
-                    start=True,
-                    stop=True,
-                )
+            nc.tensor.matmul_mx(
+                out=a_bank[e][:],
+                lhsT=words.bitcast(FP8X4),
+                lhsT_scale=scales,
+                rhs=w1[e].bitcast(FP4X4),
+                rhs_scale=w1_planes[e // SCALE_EXPERTS][:, e % SCALE_EXPERTS, :],
+                start=True,
+                stop=True,
+            )
 
         def relu(e):
             relu_out[e] = ring.tile([C, PACK, P], F32, name="relu_out")
@@ -313,33 +310,27 @@ def tile_moe_tk_mlp_relu2_kernel(
             if k >= BACK_LAG:
                 turn_back(*picks[k - BACK_LAG])
 
-        products, partial = {}, {}
-
-        def product(t0, r):
-            products[t0, r] = held.tile([P, P], F32, name=f"product{t0}_{r}")
+        def product(r, t0, t1):
+            tile = held.tile([P, t1 - t0], F32, name=f"product{r}_{t0}")
             nc.vector.tensor_tensor(
-                products[t0, r][:],
-                y[:].indirect(pos_sb[r][:, list_columns(t0, t0 + P)]),
-                gate_rows[:, r, t0 - TURNED : t0 - TURNED + P],
+                tile[:],
+                y[:].indirect(pos_sb[r][:, list_columns(t0, t1)]),
+                gate_rows[:, r, t0 - TURNED : t1 - TURNED],
                 ALU.mult,
             )
+            return tile
 
-        def add_first_two(t0):
-            partial[t0] = sums.tile([P, P], F32, name="partial")
-            nc.vector.tensor_tensor(partial[t0][:], products[t0, 0][:], products[t0, 1][:], ALU.add)
-
-        def add_third_and_store(t0):
+        def add_third_and_store(t0, third):
             total = sums.tile([P, P], F32, name="total")
-            nc.vector.tensor_tensor(total[:], partial[t0][:], products[t0, 2][:], ALU.add)
+            nc.vector.tensor_tensor(total[:], first_two[:, t0 - TURNED : t0 - TURNED + P], third[:], ALU.add)
             nc.sync.dma_start(out[:, t0 : t0 + P], total[:])
 
-        first, second = range(TURNED, T, P)
-        for r in range(TOP):
-            product(first, r)
-        product(second, 0)
-        add_first_two(first)
-        product(second, 1)
-        product(second, 2)
-        add_first_two(second)
-        add_third_and_store(first)
-        add_third_and_store(second)
+        middle = TURNED + P
+        first_choice = product(0, TURNED, T)
+        second_choice = product(1, TURNED, T)
+        third_low = product(2, TURNED, middle)
+        first_two = held.tile([P, T - TURNED], F32, name="first_two")
+        nc.vector.tensor_tensor(first_two[:], first_choice[:], second_choice[:], ALU.add)
+        third_high = product(2, middle, T)
+        add_third_and_store(TURNED, third_low)
+        add_third_and_store(middle, third_high)

@@ -38,7 +38,8 @@ X_COPIES = [
     (960, 1024, "scalar"),
 ]
 SCALE_EXPERTS = 8
-VECTOR_RELU_FROM = 3
+GPSIMD_PAIRS = 10
+VECTOR_RELUS = (19, 20, 21, 23)
 H_GROUPS = [0, 8, 16, 20, 22, 23, 24]
 Y_GROUPS = [0, 4, 8, 12, 16, 20, 23, 24]
 VECTOR_Y_EVERY = 8
@@ -52,12 +53,22 @@ W1_ROW = 2 * H
 ROUNDED_AT = {896: 0, 960: 4 * W1_ROW}
 LATE_W1_AT = {(4, 8): ROUNDED_AT[896], (8, 16): ROUNDED_AT[960]}
 LAST_W1_AT = {(16, 20): 12 * W1_ROW, (20, 24): 16 * W1_ROW}
-H_WORDS_AT = {0: LAST_W1_AT[16, 20], 8: LAST_W1_AT[20, 24]}
+H_WORDS_AT = {0: LAST_W1_AT[20, 24] - 2 * W1_ROW, 8: LAST_W1_AT[20, 24] + 2 * W1_ROW}
+Y_BANKS = [3, 2, 6, 7, 4, 5, 0]
 
 
 def relu_on_vector(e):
-    pair = e // 2
-    return pair == PAIRS - 1 or (e % 2 == 1 and pair >= VECTOR_RELU_FROM)
+    return e in VECTOR_RELUS
+
+
+def squared_on_gpsimd(e):
+    return e % 2 == 0 and e // 2 < GPSIMD_PAIRS
+
+
+def turn_bank(e):
+    if e // 2 < GPSIMD_PAIRS:
+        return RING + (e // 2) % RING
+    return {20: 6, 21: 7, 22: 0, 23: 1}[e]
 
 
 def group_of(e, bounds):
@@ -174,6 +185,7 @@ def tile_moe_tk_mlp_relu2_kernel(
             load_words(nc.scalar, w1, w1_words, W1_ROW, a, b, f"w1_{a}", at)
 
         gathered, a_bank, relu_out, turned_a, h, h_codes = {}, {}, {}, {}, {}, {}
+        squared = {}
 
         def gather(e):
             if e >= 2 and e % 2 == 1:
@@ -202,23 +214,48 @@ def tile_moe_tk_mlp_relu2_kernel(
 
         def relu(e):
             relu_out[e] = ring.tile([C, PACK, P], F32, name="relu_out")
-            src = a_bank[e][:].rearrange("s (m t) -> s t m", t=PACK)
-            if relu_on_vector(e):
-                nc.vector.tensor_scalar_max(relu_out[e][:], src, 0.0)
+            if squared_on_gpsimd(e):
+                src = a_bank[e][:].rearrange("s (m u d) -> s u m d", u=2, d=2)
+                dst = relu_out[e][:].rearrange("s t m -> s (t m)").rearrange("s (u m d) -> s u m d", u=2, d=2)
             else:
-                nc.scalar.activation(relu_out[e][:], src, ACT.Relu)
+                src = a_bank[e][:].rearrange("s (m t) -> s t m", t=PACK)
+                dst = relu_out[e][:]
+            if relu_on_vector(e):
+                nc.vector.tensor_scalar_max(dst, src, 0.0)
+            else:
+                nc.scalar.activation(dst, src, ACT.Relu)
+            if squared_on_gpsimd(e):
+                flat = relu_out[e][:].rearrange("s t m -> s (t m)")
+                squared[e] = ring.tile([C, H], BF16, name="squared")
+                nc.gpsimd.tensor_tensor(squared[e][:], flat, flat, ALU.mult)
+
+        def h_tile(e):
+            first, end = group_of(e, H_GROUPS)
+            if first not in h:
+                h[first] = held.tile([P, end - first, C, PACK], BF16, name=f"h{first}", align_bytes=64)
+            return h[first][:, e - first]
 
         def turn(e):
-            turned_a[e] = in_bank(RING + e % RING, [P, PACK, C], f"turned_a{e}")
+            if squared_on_gpsimd(e):
+                return
+            turned_a[e] = in_bank(turn_bank(e), [P, PACK, C], f"turned_a{e}")
             for t in range(PACK):
                 nc.tensor.transpose(turned_a[e][:, t, :], relu_out[e][:, t, :], ident[:])
 
+        def turn_words(e):
+            if not squared_on_gpsimd(e):
+                return
+            turned = in_bank(turn_bank(e), [P, 2, C], f"turned_w{e}")
+            words = squared[e][:].bitcast(F32)
+            for u in range(2):
+                nc.tensor.transpose(turned[:, u, :], words[:, u * P : (u + 1) * P], ident[:])
+            nc.vector.tensor_copy(h_tile(e).bitcast(F32), turned[:].rearrange("p u s -> p s u"))
+
         def square(e):
-            first, end = group_of(e, H_GROUPS)
-            if e == first:
-                h[first] = held.tile([P, end - first, C, PACK], BF16, name=f"h{first}", align_bytes=64)
+            if squared_on_gpsimd(e):
+                return
             src = turned_a[e][:].rearrange("p t (c i) -> p c t i", i=4)
-            dst = h[first][:, e - first].rearrange("p (c i) t -> p c t i", i=4)
+            dst = h_tile(e).rearrange("p (c i) t -> p c t i", i=4)
             nc.scalar.activation(dst, src, ACT.Square)
 
         def quantise(first):
@@ -234,14 +271,14 @@ def tile_moe_tk_mlp_relu2_kernel(
                 cols = slice((e - first) * C, (e - first + 1) * C)
                 h_codes[e] = (words[:, cols], scales[:, cols])
 
-        stages = [(relu, 0), (first_product, -1), (square, 1), (gather, -2), (turn, 0)]
+        stages = [(relu, 0), (first_product, -1), (square, 1), (gather, -2), (turn, 0), (turn_words, 1)]
         for step in range(min(lag for stage, lag in stages), PAIRS):
             for stage, lag in stages:
                 if 0 <= step - lag < PAIRS:
                     stage(2 * (step - lag))
                     stage(2 * (step - lag) + 1)
 
-        for first in (H_GROUPS[2], H_GROUPS[0], H_GROUPS[1]):
+        for first in H_GROUPS[:3]:
             quantise(first)
         square(E - 2)
         square(E - 1)
@@ -249,7 +286,7 @@ def tile_moe_tk_mlp_relu2_kernel(
             quantise(first)
 
         for g, (lo, hi) in enumerate(zip(Y_GROUPS, Y_GROUPS[1:])):
-            y_bank = in_bank(g, [N, 4, C], f"y_bank{g}")
+            y_bank = in_bank(Y_BANKS[g], [N, 4, C], f"y_bank{g}")
             for e in range(lo, hi):
                 words, scales = h_codes[e]
                 nc.tensor.matmul_mx(

@@ -43,8 +43,8 @@ VECTOR_RELUS = (19, 20, 21, 23)
 H_GROUPS = [0, 8, 16, 20, 22, 23, 24]
 Y_GROUPS = [0, 4, 8, 12, 16, 20, 23, 24]
 VECTOR_Y_EVERY = 8
-TURNED = 768
-TURNED_GROUP = TURNED // 2
+TURNED = 384
+TURNED_GROUP = TURNED
 TURNED_BLOCKS = TURNED_GROUP // P
 TURN_BANKS = 3
 BACK_LAG = 2
@@ -88,7 +88,6 @@ def tile_moe_tk_mlp_relu2_kernel(
         held = ctx.enter_context(tc.tile_pool(name="held", bufs=1))
         shared = ctx.enter_context(tc.tile_pool(name="shared", bufs=1))
         ring = ctx.enter_context(tc.tile_pool(name="ring", bufs=6))
-        sums = ctx.enter_context(tc.tile_pool(name="sums", bufs=2))
         gath = ctx.enter_context(tc.tile_pool(name="gath", bufs=3))
         psum = ctx.enter_context(tc.psum_pool(name="psum", bufs=1))
 
@@ -309,7 +308,7 @@ def tile_moe_tk_mlp_relu2_kernel(
         def pick_turn_gate(group, r):
             t0 = group * TURNED_GROUP
             picked = held.tile([P, TURNED_GROUP], F32, name=f"picked{group}_{r}")
-            nc.vector.tensor_copy(picked[:], y[:].indirect(pos_sb[r][:, list_columns(t0, t0 + TURNED_GROUP)]))
+            nc.scalar.activation(picked[:], y[:].indirect(pos_sb[r][:, list_columns(t0, t0 + TURNED_GROUP)]), ACT.Copy)
             turned_y = in_bank((group * TOP + r) % TURN_BANKS, [P, TURNED_BLOCKS, P], f"turned_y{group}_{r}")
             for c in range(TURNED_BLOCKS):
                 nc.tensor.transpose(turned_y[:, c, :], picked[:, c * P : (c + 1) * P], ident[:])
@@ -357,17 +356,22 @@ def tile_moe_tk_mlp_relu2_kernel(
             )
             return tile
 
-        def add_third_and_store(t0, third):
-            total = sums.tile([P, P], F32, name="total")
-            nc.vector.tensor_tensor(total[:], first_two[:, t0 - TURNED : t0 - TURNED + P], third[:], ALU.add)
-            nc.sync.dma_start(out[:, t0 : t0 + P], total[:])
+        def add(t0, t1, left, right, name):
+            tile = held.tile([P, t1 - t0], F32, name=f"{name}{t0}")
+            nc.vector.tensor_tensor(tile[:], left, right, ALU.add)
+            return tile
 
-        middle = TURNED + P
-        first_choice = product(0, TURNED, T)
-        second_choice = product(1, TURNED, T)
-        third_low = product(2, TURNED, middle)
-        first_two = held.tile([P, T - TURNED], F32, name="first_two")
-        nc.vector.tensor_tensor(first_two[:], first_choice[:], second_choice[:], ALU.add)
+        split = T - 2 * P
+        middle = T - P
+        early = [product(r, TURNED, split) for r in range(TOP)]
+        early_two = add(TURNED, split, early[0][:], early[1][:], "two")
+        first_choice = product(0, split, T)
+        early_sum = add(TURNED, split, early_two[:], early[2][:], "total")
+        nc.sync.dma_start(out[:, TURNED:split], early_sum[:])
+        second_choice = product(1, split, T)
+        third_low = product(2, split, middle)
+        first_two = add(split, T, first_choice[:], second_choice[:], "two")
         third_high = product(2, middle, T)
-        add_third_and_store(TURNED, third_low)
-        add_third_and_store(middle, third_high)
+        for t0, third in ((split, third_low), (middle, third_high)):
+            total = add(t0, t0 + P, first_two[:, t0 - split : t0 - split + P], third[:], "total")
+            nc.sync.dma_start(out[:, t0 : t0 + P], total[:])

@@ -39,9 +39,9 @@ X_COPIES = [
 ]
 SCALE_EXPERTS = 8
 GPSIMD_PAIRS = 10
-VECTOR_RELUS = (19, 20, 21, 23)
-H_GROUPS = [0, 8, 16, 20, 22, 23, 24]
-Y_GROUPS = [0, 4, 8, 12, 16, 20, 23, 24]
+VECTOR_RELUS = (19, 21)
+H_GROUPS = [0, 8, 16, 20, 22, 24]
+Y_GROUPS = [0, 4, 8, 12, 16, 20, 22, 24]
 VECTOR_Y_EVERY = 8
 TURNED = 384
 TURNED_GROUP = TURNED
@@ -54,7 +54,8 @@ ROUNDED_AT = {896: 0, 960: 4 * W1_ROW}
 LATE_W1_AT = {(4, 8): ROUNDED_AT[896], (8, 16): ROUNDED_AT[960]}
 LAST_W1_AT = {(16, 20): 12 * W1_ROW, (20, 24): 16 * W1_ROW}
 H_WORDS_AT = {0: LAST_W1_AT[20, 24] - 2 * W1_ROW, 8: LAST_W1_AT[20, 24] + 2 * W1_ROW}
-Y_BANKS = [3, 2, 6, 7, 4, 5, 0]
+Y_BANKS = [3, 6, 7, 0, 1, 3, 6]
+VECTOR_Y = (2, 4, 6)
 
 
 def relu_on_vector(e):
@@ -138,7 +139,8 @@ def tile_moe_tk_mlp_relu2_kernel(
         for a, b in zip(X_LOADS, X_LOADS[1:]):
             x_raw[a] = held.tile([P, PACK, b - a], F32, name=f"x_raw{a}", align_bytes=64)
             nc.sync.dma_start(x_raw[a][:], x_view[:, :, a:b])
-        nc.sync.dma_start(offs_sb[:], offs)
+            if a == 0:
+                nc.sync.dma_start(offs_sb[:], offs)
         load_words(nc.sync, w1, w1_words, W1_ROW, 0, 2, "w1_0")
         load_w1_scales(0)
         load_words(nc.sync, w1, w1_words, W1_ROW, 2, 4, "w1_2")
@@ -277,11 +279,9 @@ def tile_moe_tk_mlp_relu2_kernel(
                     stage(2 * (step - lag))
                     stage(2 * (step - lag) + 1)
 
-        for first in H_GROUPS[:3]:
-            quantise(first)
         square(E - 2)
         square(E - 1)
-        for first in H_GROUPS[3:-1]:
+        for first in H_GROUPS[:-1]:
             quantise(first)
 
         for g, (lo, hi) in enumerate(zip(Y_GROUPS, Y_GROUPS[1:])):
@@ -298,7 +298,7 @@ def tile_moe_tk_mlp_relu2_kernel(
                     stop=True,
                 )
             src = y_bank[:, 0 : hi - lo, :].rearrange("n q s -> n (q s)")
-            if hi % VECTOR_Y_EVERY == 0:
+            if g in VECTOR_Y:
                 nc.vector.tensor_copy(y[:, lo * C : hi * C], src)
             else:
                 nc.scalar.activation(y[:, lo * C : hi * C], src, ACT.Copy)
@@ -339,6 +339,9 @@ def tile_moe_tk_mlp_relu2_kernel(
                 t0 = group * TURNED_GROUP
                 nc.scalar.dma_start(out[:, t0 : t0 + TURNED_GROUP], result[:].rearrange("n c t -> n (c t)"))
 
+        split = T - 2 * P
+        picked_third = held.tile([P, T - split], F32, name="picked_third")
+        nc.scalar.activation(picked_third[:], y[:].indirect(pos_sb[TOP - 1][:, list_columns(split, T)]), ACT.Copy)
         picks = [(group, r) for group in range(TURNED // TURNED_GROUP) for r in range(TOP)]
         for k in range(len(picks) + BACK_LAG):
             if k < len(picks):
@@ -361,17 +364,16 @@ def tile_moe_tk_mlp_relu2_kernel(
             nc.vector.tensor_tensor(tile[:], left, right, ALU.add)
             return tile
 
-        split = T - 2 * P
-        middle = T - P
         early = [product(r, TURNED, split) for r in range(TOP)]
         early_two = add(TURNED, split, early[0][:], early[1][:], "two")
         first_choice = product(0, split, T)
         early_sum = add(TURNED, split, early_two[:], early[2][:], "total")
         nc.sync.dma_start(out[:, TURNED:split], early_sum[:])
         second_choice = product(1, split, T)
-        third_low = product(2, split, middle)
+        third = held.tile([P, T - split], F32, name="third")
+        nc.vector.tensor_tensor(third[:], picked_third[:], gate_rows[:, TOP - 1, split - TURNED :], ALU.mult)
         first_two = add(split, T, first_choice[:], second_choice[:], "two")
-        third_high = product(2, middle, T)
-        for t0, third in ((split, third_low), (middle, third_high)):
-            total = add(t0, t0 + P, first_two[:, t0 - split : t0 - split + P], third[:], "total")
+        for t0 in range(split, T, P):
+            cols = slice(t0 - split, t0 - split + P)
+            total = add(t0, t0 + P, first_two[:, cols], third[:, cols], "total")
             nc.sync.dma_start(out[:, t0 : t0 + P], total[:])

@@ -39,7 +39,7 @@ X_COPIES = [
 ]
 SCALE_EXPERTS = 8
 GPSIMD_PAIRS = 10
-VECTOR_RELUS = (19, 21)
+VECTOR_RELUS = (18, 21)
 H_GROUPS = [0, 8, 16, 20, 22, 24]
 Y_GROUPS = [0, 4, 8, 12, 16, 20, 22, 24]
 VECTOR_Y_EVERY = 8
@@ -63,7 +63,7 @@ def relu_on_vector(e):
 
 
 def squared_on_gpsimd(e):
-    return e % 2 == 0 and e // 2 < GPSIMD_PAIRS
+    return e % 2 == 1 and e // 2 < GPSIMD_PAIRS
 
 
 def turn_bank(e):

@@ -22,8 +22,7 @@ ALU = mybir.AluOpType
 P = 128
 PACK = 4
 LIST_ROWS = 16
-PAIRS = E // 2
-BANKS = 8
+STEPS = E // 2
 BANK_BYTES = 2048
 RING = 4
 
@@ -38,38 +37,44 @@ X_COPIES = [
     (960, 1024, "scalar"),
 ]
 SCALE_EXPERTS = 8
-GPSIMD_PAIRS = 10
-VECTOR_RELUS = (18, 21)
+
+GPSIMD_END = 20
+GPSIMD_EXTRA = 8
+VECTOR_RELUS = (GPSIMD_END, GPSIMD_END + 1)
 H_GROUPS = [0, 8, 16, 20, 22, 24]
 Y_GROUPS = [0, 4, 8, 12, 16, 20, 22, 24]
-VECTOR_Y_EVERY = 8
+VECTOR_Y_FIRSTS = (12, 20, 22)
+
 TURNED = 384
-TURNED_GROUP = TURNED
-TURNED_BLOCKS = TURNED_GROUP // P
-TURN_BANKS = 3
+TURNED_BLOCKS = TURNED // P
 BACK_LAG = 2
 
 W1_ROW = 2 * H
 ROUNDED_AT = {896: 0, 960: 4 * W1_ROW}
-LATE_W1_AT = {(4, 8): ROUNDED_AT[896], (8, 16): ROUNDED_AT[960]}
-LAST_W1_AT = {(16, 20): 12 * W1_ROW, (20, 24): 16 * W1_ROW}
-H_WORDS_AT = {0: LAST_W1_AT[20, 24] - 2 * W1_ROW, 8: LAST_W1_AT[20, 24] + 2 * W1_ROW}
-Y_BANKS = [3, 6, 7, 0, 1, 3, 6]
-VECTOR_Y = (2, 4, 6)
-
-
-def relu_on_vector(e):
-    return e in VECTOR_RELUS
+MIDDLE_W1_AT = {(4, 8): ROUNDED_AT[896], (8, 16): ROUNDED_AT[960]}
+LAST_W1_LOADS = [16, 20, 24]
+H_WORDS_AT = {0: 12 * W1_ROW, 8: 16 * W1_ROW}
+LAST_RELU_AT = {GPSIMD_END - 1: H_WORDS_AT[8] - W1_ROW}
 
 
 def squared_on_gpsimd(e):
-    return e % 2 == 1 and e // 2 < GPSIMD_PAIRS
+    return e == GPSIMD_EXTRA or (e % 2 == 1 and e < GPSIMD_END)
 
 
 def turn_bank(e):
-    if e // 2 < GPSIMD_PAIRS:
-        return RING + (e // 2) % RING
-    return {20: 6, 21: 7, 22: 0, 23: 1}[e]
+    if e < E - 2:
+        return RING + len([k for k in range(e) if not squared_on_gpsimd(k)]) % RING
+    return (e - 2) % RING
+
+
+def pairs_follow(e):
+    even = e - e % 2
+    return even + 2 if GPSIMD_EXTRA <= e < GPSIMD_EXTRA + 4 else even
+
+
+def y_banks():
+    latest = [e for e in range(E - 1) if not squared_on_gpsimd(e)][-(len(Y_GROUPS) - 3) :]
+    return [(E - 1) % RING, (E - 2) % RING] + [turn_bank(e) for e in latest]
 
 
 def group_of(e, bounds):
@@ -88,7 +93,7 @@ def tile_moe_tk_mlp_relu2_kernel(
     with ExitStack() as ctx:
         held = ctx.enter_context(tc.tile_pool(name="held", bufs=1))
         shared = ctx.enter_context(tc.tile_pool(name="shared", bufs=1))
-        ring = ctx.enter_context(tc.tile_pool(name="ring", bufs=6))
+        ring = ctx.enter_context(tc.tile_pool(name="ring", bufs=8))
         gath = ctx.enter_context(tc.tile_pool(name="gath", bufs=3))
         psum = ctx.enter_context(tc.psum_pool(name="psum", bufs=1))
 
@@ -113,9 +118,10 @@ def tile_moe_tk_mlp_relu2_kernel(
         y = held.tile([P, S], F32, name="y")
         ident = held.tile([P, P], F32, name="ident")
 
-        for tile in (w1_planes[0], x_scales, w1_planes[1], w1_planes[2], w2_plane):
+        for tile in (w1_planes[0], x_scales, w1_planes[1], w1_planes[2]):
             nc.vector.memset(tile[:].bitcast(I32), 0)
         make_identity(nc, ident[:])
+        nc.gpsimd.memset(w2_plane[:].bitcast(I32), 0)
 
         w1, w2, x_raw = {}, {}, {}
 
@@ -139,15 +145,15 @@ def tile_moe_tk_mlp_relu2_kernel(
         for a, b in zip(X_LOADS, X_LOADS[1:]):
             x_raw[a] = held.tile([P, PACK, b - a], F32, name=f"x_raw{a}", align_bytes=64)
             nc.sync.dma_start(x_raw[a][:], x_view[:, :, a:b])
-            if a == 0:
+            if a == X_LOADS[0]:
                 nc.sync.dma_start(offs_sb[:], offs)
         load_words(nc.sync, w1, w1_words, W1_ROW, 0, 2, "w1_0")
         load_w1_scales(0)
         load_words(nc.sync, w1, w1_words, W1_ROW, 2, 4, "w1_2")
         load_w1_scales(1)
         load_w1_scales(2)
-        for (a, b), at in LAST_W1_AT.items():
-            load_words(nc.sync, w1, w1_words, W1_ROW, a, b, f"w1_{a}", at)
+        for a, b in zip(LAST_W1_LOADS, LAST_W1_LOADS[1:]):
+            load_words(nc.sync, w1, w1_words, W1_ROW, a, b, f"w1_{a}")
         load_scales(w2_plane, w2_scales)
         load_words(nc.sync, w2, w2_words, 2 * N, 0, E, "w2")
         for r, pos in enumerate((pos1, pos2, pos3)):
@@ -182,11 +188,10 @@ def tile_moe_tk_mlp_relu2_kernel(
             if k > 0:
                 quantise_tokens(*X_COPIES[k - 1][:2])
 
-        for (a, b), at in LATE_W1_AT.items():
+        for (a, b), at in MIDDLE_W1_AT.items():
             load_words(nc.scalar, w1, w1_words, W1_ROW, a, b, f"w1_{a}", at)
 
-        gathered, a_bank, relu_out, turned_a, h, h_codes = {}, {}, {}, {}, {}, {}
-        squared = {}
+        gathered, a_bank, relu_out, squared, turned_a, h, h_codes = {}, {}, {}, {}, {}, {}, {}
 
         def gather(e):
             if e >= 2 and e % 2 == 1:
@@ -214,14 +219,17 @@ def tile_moe_tk_mlp_relu2_kernel(
             )
 
         def relu(e):
-            relu_out[e] = ring.tile([C, PACK, P], F32, name="relu_out")
+            if e in LAST_RELU_AT:
+                relu_out[e] = placed([C, PACK, P], F32, "last_relu_out", LAST_RELU_AT[e])
+            else:
+                relu_out[e] = ring.tile([C, PACK, P], F32, name="relu_out")
             if squared_on_gpsimd(e):
                 src = a_bank[e][:].rearrange("s (m u d) -> s u m d", u=2, d=2)
                 dst = relu_out[e][:].rearrange("s t m -> s (t m)").rearrange("s (u m d) -> s u m d", u=2, d=2)
             else:
                 src = a_bank[e][:].rearrange("s (m t) -> s t m", t=PACK)
                 dst = relu_out[e][:]
-            if relu_on_vector(e):
+            if e in VECTOR_RELUS:
                 nc.vector.tensor_scalar_max(dst, src, 0.0)
             else:
                 nc.scalar.activation(dst, src, ACT.Relu)
@@ -243,14 +251,17 @@ def tile_moe_tk_mlp_relu2_kernel(
             for t in range(PACK):
                 nc.tensor.transpose(turned_a[e][:, t, :], relu_out[e][:, t, :], ident[:])
 
-        def turn_words(e):
-            if not squared_on_gpsimd(e):
+        def turn_pairs(leader):
+            followers = [e for e in range(E) if squared_on_gpsimd(e) and pairs_follow(e) == leader]
+            if not followers:
                 return
-            turned = in_bank(turn_bank(e), [P, 2, C], f"turned_w{e}")
-            words = squared[e][:].bitcast(F32)
-            for u in range(2):
-                nc.tensor.transpose(turned[:, u, :], words[:, u * P : (u + 1) * P], ident[:])
-            nc.vector.tensor_copy(h_tile(e).bitcast(F32), turned[:].rearrange("p u s -> p s u"))
+            turned = in_bank(turn_bank(leader), [P, 2, 2, C], f"turned_pairs{leader}")
+            for k, e in enumerate(followers):
+                pairs = squared[e][:].bitcast(F32)
+                for u in range(2):
+                    nc.tensor.transpose(turned[:, k, u, :], pairs[:, u * P : (u + 1) * P], ident[:])
+            for k, e in enumerate(followers):
+                nc.vector.tensor_copy(h_tile(e).bitcast(F32), turned[:, k].rearrange("p u s -> p s u"))
 
         def square(e):
             if squared_on_gpsimd(e):
@@ -272,10 +283,10 @@ def tile_moe_tk_mlp_relu2_kernel(
                 cols = slice((e - first) * C, (e - first + 1) * C)
                 h_codes[e] = (words[:, cols], scales[:, cols])
 
-        stages = [(relu, 0), (first_product, -1), (square, 1), (gather, -2), (turn, 0), (turn_words, 1)]
-        for step in range(min(lag for stage, lag in stages), PAIRS):
+        stages = [(relu, 0), (first_product, -1), (square, 1), (gather, -2), (turn, 0), (turn_pairs, 1)]
+        for step in range(min(lag for stage, lag in stages), STEPS):
             for stage, lag in stages:
-                if 0 <= step - lag < PAIRS:
+                if 0 <= step - lag < STEPS:
                     stage(2 * (step - lag))
                     stage(2 * (step - lag) + 1)
 
@@ -284,8 +295,8 @@ def tile_moe_tk_mlp_relu2_kernel(
         for first in H_GROUPS[:-1]:
             quantise(first)
 
-        for g, (lo, hi) in enumerate(zip(Y_GROUPS, Y_GROUPS[1:])):
-            y_bank = in_bank(Y_BANKS[g], [N, 4, C], f"y_bank{g}")
+        for bank, lo, hi in zip(y_banks(), Y_GROUPS, Y_GROUPS[1:]):
+            y_bank = in_bank(bank, [N, hi - lo, C], f"y_bank{lo}")
             for e in range(lo, hi):
                 words, scales = h_codes[e]
                 nc.tensor.matmul_mx(
@@ -297,83 +308,69 @@ def tile_moe_tk_mlp_relu2_kernel(
                     start=True,
                     stop=True,
                 )
-            src = y_bank[:, 0 : hi - lo, :].rearrange("n q s -> n (q s)")
-            if g in VECTOR_Y:
+            src = y_bank[:].rearrange("n q s -> n (q s)")
+            if lo in VECTOR_Y_FIRSTS:
                 nc.vector.tensor_copy(y[:, lo * C : hi * C], src)
             else:
                 nc.scalar.activation(y[:, lo * C : hi * C], src, ACT.Copy)
 
-        gated, back = {}, {}
+        def picks(r, t0, t1):
+            return y[:].indirect(pos_sb[r][:, list_columns(t0, t1)])
 
-        def pick_turn_gate(group, r):
-            t0 = group * TURNED_GROUP
-            picked = held.tile([P, TURNED_GROUP], F32, name=f"picked{group}_{r}")
-            nc.scalar.activation(picked[:], y[:].indirect(pos_sb[r][:, list_columns(t0, t0 + TURNED_GROUP)]), ACT.Copy)
-            turned_y = in_bank((group * TOP + r) % TURN_BANKS, [P, TURNED_BLOCKS, P], f"turned_y{group}_{r}")
+        last_two, last = T - 2 * P, T - P
+        picked_third = held.tile([P, P], F32, name="picked_third")
+        nc.scalar.activation(picked_third[:], picks(TOP - 1, last, T), ACT.Copy)
+
+        gated = {}
+        back = {}
+
+        def pick_turn_gate(r):
+            picked = held.tile([P, TURNED], F32, name=f"picked{r}")
+            nc.scalar.activation(picked[:], picks(r, 0, TURNED), ACT.Copy)
+            turned_y = in_bank(r, [P, TURNED_BLOCKS, P], f"turned_y{r}")
             for c in range(TURNED_BLOCKS):
                 nc.tensor.transpose(turned_y[:, c, :], picked[:, c * P : (c + 1) * P], ident[:])
-            gated[group, r] = held.tile([P, TURNED_BLOCKS, P], F32, name=f"gated{group}_{r}")
+            gated[r] = held.tile([P, TURNED_BLOCKS, P], F32, name=f"gated{r}")
             for c in range(TURNED_BLOCKS):
-                block = group * TURNED_BLOCKS + c
-                nc.scalar.activation(
-                    gated[group, r][:, c, :], turned_y[:, c, :], ACT.Copy, scale=gate_turned[r][:, block : block + 1]
-                )
+                nc.scalar.activation(gated[r][:, c, :], turned_y[:, c, :], ACT.Copy, scale=gate_turned[r][:, c : c + 1])
 
-        def turn_back(group, r):
+        def turn_back(r):
             for c in range(TURNED_BLOCKS):
                 if r == 0:
-                    block = group * TURNED_BLOCKS + c
-                    back[group, c] = in_bank((TURN_BANKS + block) % BANKS, [P, P], f"back{block}")
+                    back[c] = in_bank(TOP + c, [P, P], f"back{c}")
                 nc.tensor.matmul(
-                    back[group, c][:],
-                    gated[group, r][:, c, :],
-                    ident[:],
-                    start=r == 0,
-                    stop=r == TOP - 1,
-                    is_transpose=True,
+                    back[c][:], gated[r][:, c, :], ident[:], start=r == 0, stop=r == TOP - 1, is_transpose=True
                 )
-            if r == TOP - 1:
-                result = held.tile([P, TURNED_BLOCKS, P], F32, name=f"result{group}")
-                for c in range(TURNED_BLOCKS):
-                    nc.scalar.activation(result[:, c, :], back[group, c][:], ACT.Copy)
-                t0 = group * TURNED_GROUP
-                nc.scalar.dma_start(out[:, t0 : t0 + TURNED_GROUP], result[:].rearrange("n c t -> n (c t)"))
 
-        split = T - 2 * P
-        picked_third = held.tile([P, T - split], F32, name="picked_third")
-        nc.scalar.activation(picked_third[:], y[:].indirect(pos_sb[TOP - 1][:, list_columns(split, T)]), ACT.Copy)
-        picks = [(group, r) for group in range(TURNED // TURNED_GROUP) for r in range(TOP)]
-        for k in range(len(picks) + BACK_LAG):
-            if k < len(picks):
-                pick_turn_gate(*picks[k])
+        for k in range(TOP + BACK_LAG):
+            if k < TOP:
+                pick_turn_gate(k)
             if k >= BACK_LAG:
-                turn_back(*picks[k - BACK_LAG])
+                turn_back(k - BACK_LAG)
+        result = held.tile([P, TURNED_BLOCKS, P], F32, name="result")
+        for c in range(TURNED_BLOCKS):
+            nc.scalar.activation(result[:, c, :], back[c][:], ACT.Copy)
+        nc.scalar.dma_start(out[:, 0:TURNED], result[:].rearrange("n c t -> n (c t)"))
 
-        def product(r, t0, t1):
+        def times_gate(values, r, t0, t1):
             tile = held.tile([P, t1 - t0], F32, name=f"product{r}_{t0}")
-            nc.vector.tensor_tensor(
-                tile[:],
-                y[:].indirect(pos_sb[r][:, list_columns(t0, t1)]),
-                gate_rows[:, r, t0 - TURNED : t1 - TURNED],
-                ALU.mult,
-            )
+            nc.vector.tensor_tensor(tile[:], values, gate_rows[:, r, t0 - TURNED : t1 - TURNED], ALU.mult)
             return tile
 
-        def add(t0, t1, left, right, name):
-            tile = held.tile([P, t1 - t0], F32, name=f"{name}{t0}")
+        def add(left, right, name):
+            tile = held.tile(list(left.shape), F32, name=name)
             nc.vector.tensor_tensor(tile[:], left, right, ALU.add)
             return tile
 
-        early = [product(r, TURNED, split) for r in range(TOP)]
-        early_two = add(TURNED, split, early[0][:], early[1][:], "two")
-        first_choice = product(0, split, T)
-        early_sum = add(TURNED, split, early_two[:], early[2][:], "total")
-        nc.sync.dma_start(out[:, TURNED:split], early_sum[:])
-        second_choice = product(1, split, T)
-        third = held.tile([P, T - split], F32, name="third")
-        nc.vector.tensor_tensor(third[:], picked_third[:], gate_rows[:, TOP - 1, split - TURNED :], ALU.mult)
-        first_two = add(split, T, first_choice[:], second_choice[:], "two")
-        for t0 in range(split, T, P):
-            cols = slice(t0 - split, t0 - split + P)
-            total = add(t0, t0 + P, first_two[:, cols], third[:, cols], "total")
+        early = [times_gate(picks(r, TURNED, last_two), r, TURNED, last_two) for r in range(TOP)]
+        early_two = add(early[0][:], early[1][:], "early_two")
+        late_first = times_gate(picks(0, last_two, T), 0, last_two, T)
+        early_sum = add(early_two[:], early[2][:], "early_sum")
+        nc.sync.dma_start(out[:, TURNED:last_two], early_sum[:])
+        late_second = times_gate(picks(1, last_two, T), 1, last_two, T)
+        third_low = times_gate(picks(2, last_two, last), 2, last_two, last)
+        late_two = add(late_first[:], late_second[:], "late_two")
+        third_high = times_gate(picked_third[:], 2, last, T)
+        for t0, third in ((last_two, third_low), (last, third_high)):
+            total = add(late_two[:, t0 - last_two : t0 - last_two + P], third[:], f"late_sum{t0}")
             nc.sync.dma_start(out[:, t0 : t0 + P], total[:])

@@ -147,9 +147,9 @@ def tile_moe_tk_mlp_relu2_kernel(
             nc.sync.dma_start(x_raw[a][:], x_view[:, :, a:b])
             if a == X_LOADS[0]:
                 nc.sync.dma_start(offs_sb[:], offs)
-        load_words(nc.sync, w1, w1_words, W1_ROW, 0, 2, "w1_0")
+        load_words(nc.sync, w1, w1_words, W1_ROW, 0, 1, "w1_0")
         load_w1_scales(0)
-        load_words(nc.sync, w1, w1_words, W1_ROW, 2, 4, "w1_2")
+        load_words(nc.sync, w1, w1_words, W1_ROW, 1, 4, "w1_1")
         load_w1_scales(1)
         load_w1_scales(2)
         for a, b in zip(LAST_W1_LOADS, LAST_W1_LOADS[1:]):

from contextlib import ExitStack

import concourse.mybir as mybir
from concourse.masks import make_identity

K, T, E, C, H, N = 512, 1024, 24, 128, 512, 128
TOP = 3
S = E * C
FLOPS = 2 * S * (K * H + H * N)

F32 = mybir.dt.float32
BF16 = mybir.dt.bfloat16
I32 = mybir.dt.int32
U32 = mybir.dt.uint32
U16 = mybir.dt.uint16
U8 = mybir.dt.uint8
FP8X4 = mybir.dt.float8_e4m3fn_x4
FP4X4 = mybir.dt.float4_e2m1fn_x4
ACT = mybir.ActivationFunctionType
ALU = mybir.AluOpType

P = 128
PACK = 4
LIST_ROWS = 16
STEPS = E // 2
BANK_BYTES = 2048
RING = 4

X_LOADS = [0, 512, 768, 896, 1024]
X_COPIES = [
    (256, 512, "vector"),
    (0, 256, "scalar"),
    (640, 768, "vector"),
    (512, 640, "scalar"),
    (768, 896, "scalar"),
    (896, 960, "vector"),
    (960, 1024, "scalar"),
]
SCALE_EXPERTS = 8

GPSIMD_END = 20
GPSIMD_EXTRA = 8
VECTOR_RELUS = (GPSIMD_END, GPSIMD_END + 1)
H_GROUPS = [0, 8, 16, 20, 22, 24]
Y_GROUPS = [0, 4, 8, 12, 16, 20, 22, 24]
VECTOR_Y_FIRSTS = (12, 20, 22)

TURNED = 384
TURNED_BLOCKS = TURNED // P
BACK_LAG = 2

W1_ROW = 2 * H
ROUNDED_AT = {896: 0, 960: 4 * W1_ROW}
MIDDLE_W1_AT = {(4, 8): ROUNDED_AT[896], (8, 16): ROUNDED_AT[960]}
LAST_W1_LOADS = [16, 20, 24]
H_WORDS_AT = {0: 12 * W1_ROW, 8: 16 * W1_ROW}
LAST_RELU_AT = {GPSIMD_END - 1: H_WORDS_AT[8] - W1_ROW}


def squared_on_gpsimd(e):
    return e == GPSIMD_EXTRA or (e % 2 == 1 and e < GPSIMD_END)


def turn_bank(e):
    if e < E - 2:
        return RING + len([k for k in range(e) if not squared_on_gpsimd(k)]) % RING
    return (e - 2) % RING


def pairs_follow(e):
    even = e - e % 2
    return even + 2 if GPSIMD_EXTRA <= e < GPSIMD_EXTRA + 4 else even


def y_banks():
    latest = [e for e in range(E - 1) if not squared_on_gpsimd(e)][-(len(Y_GROUPS) - 3) :]
    return [(E - 1) % RING, (E - 2) % RING] + [turn_bank(e) for e in latest]


def group_of(e, bounds):
    k = max(k for k, first in enumerate(bounds) if first <= e)
    return bounds[k], bounds[k + 1]


def list_columns(first, end):
    return slice(first // LIST_ROWS, end // LIST_ROWS)


def tile_moe_tk_mlp_relu2_kernel(
    tc, xT, w1_words, w1_scales, w2_words, w2_scales, gate, offs, pos1, pos2, pos3, out
):
    nc = tc.nc
    with ExitStack() as ctx:
        held = ctx.enter_context(tc.tile_pool(name="held", bufs=1))
        shared = ctx.enter_context(tc.tile_pool(name="shared", bufs=1))
        ring = ctx.enter_context(tc.tile_pool(name="ring", bufs=8))
        gath = ctx.enter_context(tc.tile_pool(name="gath", bufs=3))
        psum = ctx.enter_context(tc.psum_pool(name="psum", bufs=1))

        def in_bank(number, shape, name):
            return psum.tile(shape, F32, name=name, offset=number * BANK_BYTES)

        def placed(shape, dtype, name, at):
            if at is None:
                return held.tile(shape, dtype, name=name, align_bytes=64)
            return shared.tile(shape, dtype, name=name, align_bytes=64, offset=at)

        offs_sb = held.tile([P, S // LIST_ROWS], U16, name="offs_sb")
        pos_sb = [held.tile([P, T // LIST_ROWS], U16, name=f"pos{r}_sb") for r in range(TOP)]
        x_words = held.tile([P, T], U32, name="x_words", align_bytes=64)
        x_scales = held.tile([P, T], U8, name="x_scales", align_bytes=64)
        w1_planes = [
            held.tile([P, SCALE_EXPERTS, H], U8, name=f"w1s{a}", align_bytes=64) for a in range(0, E, SCALE_EXPERTS)
        ]
        w2_plane = held.tile([P, E, N], U8, name="w2s", align_bytes=64)
        gate_rows = held.tile([P, TOP, T - TURNED], F32, name="gate_rows")
        gate_turned = [held.tile([P, TURNED // P], F32, name=f"gate_turned{r}") for r in range(TOP)]
        y = held.tile([P, S], F32, name="y")
        ident = held.tile([P, P], F32, name="ident")

        for tile in (w1_planes[0], x_scales, w1_planes[1], w1_planes[2]):
            nc.vector.memset(tile[:].bitcast(I32), 0)
        make_identity(nc, ident[:])
        nc.gpsimd.memset(w2_plane[:].bitcast(I32), 0)

        w1, w2, x_raw = {}, {}, {}

        def load_words(queue, dst, src, width, a, b, name, at=None):
            tile = placed([P, b - a, width], U8, name, at)
            queue.dma_start(tile[:].bitcast(I32), src[a:b, 0].rearrange("e p n -> p e n").bitcast(I32))
            for e in range(a, b):
                dst[e] = tile[:, e - a, :]

        def load_scales(tile, src):
            for r in range(4):
                nc.sync.dma_start(
                    tile[r:P:32, :, :].bitcast(I32),
                    src[:, 0, r:16:4, :].rearrange("e q n -> q e n").bitcast(I32),
                )

        def load_w1_scales(k):
            load_scales(w1_planes[k], w1_scales[k * SCALE_EXPERTS : (k + 1) * SCALE_EXPERTS])

        x_view = xT.rearrange("(p j) t -> p j t", j=PACK)
        for a, b in zip(X_LOADS, X_LOADS[1:]):
            x_raw[a] = held.tile([P, PACK, b - a], F32, name=f"x_raw{a}", align_bytes=64)
            nc.sync.dma_start(x_raw[a][:], x_view[:, :, a:b])
            if a == X_LOADS[0]:
                nc.sync.dma_start(offs_sb[:], offs)
        load_words(nc.sync, w1, w1_words, W1_ROW, 0, 1, "w1_0")
        load_w1_scales(0)
        load_words(nc.sync, w1, w1_words, W1_ROW, 1, 4, "w1_1")
        load_w1_scales(1)
        load_w1_scales(2)
        for a, b in zip(LAST_W1_LOADS, LAST_W1_LOADS[1:]):
            load_words(nc.sync, w1, w1_words, W1_ROW, a, b, f"w1_{a}")
        load_scales(w2_plane, w2_scales)
        load_words(nc.sync, w2, w2_words, 2 * N, 0, E, "w2")
        for r, pos in enumerate((pos1, pos2, pos3)):
            nc.sync.dma_start(pos_sb[r][:], pos)
        nc.sync.dma_start(gate_rows[:], gate[:, :, TURNED:T].rearrange("r p t -> p r t"))
        with nc.allow_non_contiguous_dma(reason="one gate value a partition"):
            for r in range(TOP):
                nc.sync.dma_start(gate_turned[r][:], gate[r, 0, 0:TURNED].rearrange("(b p) -> p b", p=P))

        rounded = {}

        def round_tokens(t0, t1, engine):
            rounded[t0] = placed([P, t1 - t0, PACK], BF16, f"x_rounded{t0}", ROUNDED_AT.get(t0))
            lo = max(a for a in X_LOADS if a <= t0)
            src = x_raw[lo][:, :, t0 - lo : t1 - lo].rearrange("p j (c i) -> p c j i", i=4)
            dst = rounded[t0][:].rearrange("p (c i) j -> p c j i", i=4)
            if engine == "scalar":
                nc.scalar.activation(dst, src, ACT.Copy)
            else:
                nc.vector.tensor_copy(dst, src)

        def quantise_tokens(t0, t1):
            nc.vector.quantize_mx(
                out=x_words[:, t0:t1].bitcast(FP8X4),
                scales=x_scales[:, t0:t1],
                in_=rounded[t0][:].rearrange("p t j -> p (t j)"),
            )

        for k in range(len(X_COPIES) + 1):
            if k < len(X_COPIES):
                round_tokens(*X_COPIES[k])
            if k > 0:
                quantise_tokens(*X_COPIES[k - 1][:2])

        for (a, b), at in MIDDLE_W1_AT.items():
            load_words(nc.scalar, w1, w1_words, W1_ROW, a, b, f"w1_{a}", at)

        gathered, a_bank, relu_out, squared, turned_a, h, h_codes = {}, {}, {}, {}, {}, {}, {}

        def gather(e):
            if e >= 2 and e % 2 == 1:
                return
            count = 1 if e < 2 else 2
            entries = offs_sb[:, list_columns(e * C, (e + count) * C)]
            words = gath.tile([P, count * C], U32, name="slot_words", align_bytes=64)
            scales = gath.tile([P, count * C], U8, name="slot_scales", align_bytes=64)
            nc.vector.tensor_copy(words[:], x_words[:].indirect(entries))
            nc.vector.tensor_copy(scales[:], x_scales[:].indirect(entries))
            for k in range(count):
                gathered[e + k] = (words[:, k * C : (k + 1) * C], scales[:, k * C : (k + 1) * C])

        def first_product(e):
            words, scales = gathered[e]
            a_bank[e] = in_bank(e % RING, [C, H], f"a{e}")
            nc.tensor.matmul_mx(
                out=a_bank[e][:],
                lhsT=words.bitcast(FP8X4),
                lhsT_scale=scales,
                rhs=w1[e].bitcast(FP4X4),
                rhs_scale=w1_planes[e // SCALE_EXPERTS][:, e % SCALE_EXPERTS, :],
                start=True,
                stop=True,
            )

        def relu(e):
            if e in LAST_RELU_AT:
                relu_out[e] = placed([C, PACK, P], F32, "last_relu_out", LAST_RELU_AT[e])
            else:
                relu_out[e] = ring.tile([C, PACK, P], F32, name="relu_out")
            if squared_on_gpsimd(e):
                src = a_bank[e][:].rearrange("s (m u d) -> s u m d", u=2, d=2)
                dst = relu_out[e][:].rearrange("s t m -> s (t m)").rearrange("s (u m d) -> s u m d", u=2, d=2)
            else:
                src = a_bank[e][:].rearrange("s (m t) -> s t m", t=PACK)
                dst = relu_out[e][:]
            if e in VECTOR_RELUS:
                nc.vector.tensor_scalar_max(dst, src, 0.0)
            else:
                nc.scalar.activation(dst, src, ACT.Relu)
            if squared_on_gpsimd(e):
                flat = relu_out[e][:].rearrange("s t m -> s (t m)")
                squared[e] = ring.tile([C, H], BF16, name="squared")
                nc.gpsimd.tensor_tensor(squared[e][:], flat, flat, ALU.mult)

        def h_tile(e):
            first, end = group_of(e, H_GROUPS)
            if first not in h:
                h[first] = held.tile([P, end - first, C, PACK], BF16, name=f"h{first}", align_bytes=64)
            return h[first][:, e - first]

        def turn(e):
            if squared_on_gpsimd(e):
                return
            turned_a[e] = in_bank(turn_bank(e), [P, PACK, C], f"turned_a{e}")
            for t in range(PACK):
                nc.tensor.transpose(turned_a[e][:, t, :], relu_out[e][:, t, :], ident[:])

        def turn_pairs(leader):
            followers = [e for e in range(E) if squared_on_gpsimd(e) and pairs_follow(e) == leader]
            if not followers:
                return
            turned = in_bank(turn_bank(leader), [P, 2, 2, C], f"turned_pairs{leader}")
            for k, e in enumerate(followers):
                pairs = squared[e][:].bitcast(F32)
                for u in range(2):
                    nc.tensor.transpose(turned[:, k, u, :], pairs[:, u * P : (u + 1) * P], ident[:])
            for k, e in enumerate(followers):
                nc.vector.tensor_copy(h_tile(e).bitcast(F32), turned[:, k].rearrange("p u s -> p s u"))

        def square(e):
            if squared_on_gpsimd(e):
                return
            src = turned_a[e][:].rearrange("p t (c i) -> p c t i", i=4)
            dst = h_tile(e).rearrange("p (c i) t -> p c t i", i=4)
            nc.scalar.activation(dst, src, ACT.Square)

        def quantise(first):
            end = group_of(first, H_GROUPS)[1]
            words = placed([P, (end - first) * C], U32, f"h_words{first}", H_WORDS_AT.get(first))
            scales = held.tile([P, (end - first) * C], U8, name=f"h_scales{first}", align_bytes=64)
            nc.vector.quantize_mx(
                out=words[:].bitcast(FP8X4),
                scales=scales[:],
                in_=h[first][:].rearrange("p e s t -> p (e s t)"),
            )
            for e in range(first, end):
                cols = slice((e - first) * C, (e - first + 1) * C)
                h_codes[e] = (words[:, cols], scales[:, cols])

        stages = [(relu, 0), (first_product, -1), (square, 1), (gather, -2), (turn, 0), (turn_pairs, 1)]
        for step in range(min(lag for stage, lag in stages), STEPS):
            for stage, lag in stages:
                if 0 <= step - lag < STEPS:
                    stage(2 * (step - lag))
                    stage(2 * (step - lag) + 1)

        square(E - 2)
        square(E - 1)
        for first in H_GROUPS[:-1]:
            quantise(first)

        for bank, lo, hi in zip(y_banks(), Y_GROUPS, Y_GROUPS[1:]):
            y_bank = in_bank(bank, [N, hi - lo, C], f"y_bank{lo}")
            for e in range(lo, hi):
                words, scales = h_codes[e]
                nc.tensor.matmul_mx(
                    out=y_bank[:, e - lo, :],
                    lhsT=w2[e].bitcast(FP4X4),
                    lhsT_scale=w2_plane[:, e, :],
                    rhs=words.bitcast(FP8X4),
                    rhs_scale=scales,
                    start=True,
                    stop=True,
                )
            src = y_bank[:].rearrange("n q s -> n (q s)")
            if lo in VECTOR_Y_FIRSTS:
                nc.vector.tensor_copy(y[:, lo * C : hi * C], src)
            else:
                nc.scalar.activation(y[:, lo * C : hi * C], src, ACT.Copy)

        def picks(r, t0, t1):
            return y[:].indirect(pos_sb[r][:, list_columns(t0, t1)])

        last_two, last = T - 2 * P, T - P
        picked_third = held.tile([P, P], F32, name="picked_third")
        nc.scalar.activation(picked_third[:], picks(TOP - 1, last, T), ACT.Copy)

        gated = {}
        back = {}

        def pick_turn_gate(r):
            picked = held.tile([P, TURNED], F32, name=f"picked{r}")
            nc.scalar.activation(picked[:], picks(r, 0, TURNED), ACT.Copy)
            turned_y = in_bank(r, [P, TURNED_BLOCKS, P], f"turned_y{r}")
            for c in range(TURNED_BLOCKS):
                nc.tensor.transpose(turned_y[:, c, :], picked[:, c * P : (c + 1) * P], ident[:])
            gated[r] = held.tile([P, TURNED_BLOCKS, P], F32, name=f"gated{r}")
            for c in range(TURNED_BLOCKS):
                nc.scalar.activation(gated[r][:, c, :], turned_y[:, c, :], ACT.Copy, scale=gate_turned[r][:, c : c + 1])

        def turn_back(r):
            for c in range(TURNED_BLOCKS):
                if r == 0:
                    back[c] = in_bank(TOP + c, [P, P], f"back{c}")
                nc.tensor.matmul(
                    back[c][:], gated[r][:, c, :], ident[:], start=r == 0, stop=r == TOP - 1, is_transpose=True
                )

        for k in range(TOP + BACK_LAG):
            if k < TOP:
                pick_turn_gate(k)
            if k >= BACK_LAG:
                turn_back(k - BACK_LAG)
        result = held.tile([P, TURNED_BLOCKS, P], F32, name="result")
        for c in range(TURNED_BLOCKS):
            nc.scalar.activation(result[:, c, :], back[c][:], ACT.Copy)
        nc.scalar.dma_start(out[:, 0:TURNED], result[:].rearrange("n c t -> n (c t)"))

        def times_gate(values, r, t0, t1):
            tile = held.tile([P, t1 - t0], F32, name=f"product{r}_{t0}")
            nc.vector.tensor_tensor(tile[:], values, gate_rows[:, r, t0 - TURNED : t1 - TURNED], ALU.mult)
            return tile

        def add(left, right, name):
            tile = held.tile(list(left.shape), F32, name=name)
            nc.vector.tensor_tensor(tile[:], left, right, ALU.add)
            return tile

        early = [times_gate(picks(r, TURNED, last_two), r, TURNED, last_two) for r in range(TOP)]
        early_two = add(early[0][:], early[1][:], "early_two")
        late_first = times_gate(picks(0, last_two, T), 0, last_two, T)
        early_sum = add(early_two[:], early[2][:], "early_sum")
        nc.sync.dma_start(out[:, TURNED:last_two], early_sum[:])
        late_second = times_gate(picks(1, last_two, T), 1, last_two, T)
        third_low = times_gate(picks(2, last_two, last), 2, last_two, last)
        late_two = add(late_first[:], late_second[:], "late_two")
        third_high = times_gate(picked_third[:], 2, last, T)
        for t0, third in ((last_two, third_low), (last, third_high)):
            total = add(late_two[:, t0 - last_two : t0 - last_two + P], third[:], f"late_sum{t0}")
            nc.sync.dma_start(out[:, t0 : t0 + P], total[:])
